import numpy as np
import ml_dtypes


def mxq(x, axis, fmt="e4m3"):
    dtype, down = {"e4m3": (ml_dtypes.float8_e4m3fn, 7), "e5m2": (ml_dtypes.float8_e5m2, 14)}[fmt]
    v = np.moveaxis(np.asarray(x, np.float32).astype(ml_dtypes.bfloat16).astype(np.float64), axis, -1)
    blocks = v.reshape(v.shape[:-1] + (-1, 32))
    amax = np.abs(blocks).max(-1, keepdims=True)
    byte = np.maximum(np.where(amax > 0, np.frexp(amax)[1] - 1 + 127, 0) - down, 1)
    scale = np.exp2(byte - 127.0)
    codes = (blocks / scale).astype(np.float32).astype(dtype).astype(np.float64)
    return np.moveaxis((codes * scale).reshape(v.shape), -1, axis)


WIDE = False


def mx_kscale(k):
    if not WIDE:
        return np.ones(k)
    levels = np.array([10, -10, 5, -5, 0])
    if k % 512:
        return np.exp2(np.random.permutation(np.resize(levels, k // 32))).repeat(32)
    a = np.empty((k // 512, 16))
    for p in range(k // 512):
        a[p, :8] = np.random.permutation(np.resize(levels, 8))
        for g in range(8):
            far = levels[np.abs(levels - a[p, g]) >= 10]
            a[p, g + 8] = far[np.random.randint(len(far))]
    return np.exp2(a.ravel()).repeat(32)


def f64(x):
    return np.asarray(x).astype(np.float64)


def striped(idx):
    return np.tile(idx.reshape(-1, 16).T, (8, 1)).astype(np.uint16)


def unstriped(offs):
    return offs[:16].T.reshape(-1).astype(np.int64)


def pack_weight(w):
    k, n = w.shape
    w = f64(np.asarray(w, np.float32).astype(ml_dtypes.bfloat16)).reshape(k // 32, 32, n)
    amax = np.abs(w).max(1)
    byte = np.clip(np.where(amax > 0, np.frexp(amax)[1] - 1 + 127 - 7, 1), 1, 254)
    scaled = (w * np.exp2(127.0 - byte)[:, None, :]).reshape(k, n).astype(np.float32)
    words = np.ascontiguousarray(scaled.reshape(k // 512, 128, 4, n).transpose(0, 1, 3, 2)).astype(ml_dtypes.float8_e4m3fn).view(np.uint8)
    return words, np.ascontiguousarray(byte.astype(np.uint8).reshape(k // 512, 16, n))


def unpack_weight(words, scales):
    g, p, n, _ = words.shape
    vals = np.ascontiguousarray(words).view(ml_dtypes.float8_e4m3fn).astype(np.float64) * np.repeat(np.exp2(scales.astype(np.float64) - 127.0), 8, axis=1)[..., None]
    return vals.transpose(0, 1, 3, 2).reshape(g * 512, n)


K, T, E, C, N = 2560, 1024, 4, 128, 256


def by_expert(wq, xq):
    return np.concatenate([wq[e].T @ xq[:, e * C:(e + 1) * C] for e in range(E)], axis=1)


def setup_inputs():
    n = np.random.standard_normal
    s = mx_kscale(K)[:, None]
    packed = [pack_weight(m) for m in n((E, K, N)) / np.sqrt(K) / s[None]]
    return {
        "xT": (n((K, T)) * s).astype(np.float32),
        "xr": n((N, T)).astype(np.float32),
        "w_words": np.stack([m[0] for m in packed]),
        "w_scales": np.stack([m[1] for m in packed]),
        "gate": np.tile(np.random.uniform(0.2, 1.0, E * C), (N, 1)).astype(np.float32),
        "offs": striped(np.random.permutation(T)[:E * C]),
    }


def reference(xT, xr, w_words, w_scales, gate, offs):
    idx = unstriped(offs)
    w = np.stack([unpack_weight(w_words[e], w_scales[e]) for e in range(E)])
    xq = mxq(f64(xT)[:, idx], 0, "e4m3")
    y = by_expert(w, xq)
    out = f64(xr).copy()
    out[:, idx] += f64(gate) * y
    return out

@@ -1,0 +1,171 @@
+from contextlib import ExitStack
+
+import concourse.mybir as mybir
+
+K, T, E, C, N = 2560, 1024, 4, 128, 256
+SLOTS = E * C
+FLOPS = 2 * K * SLOTS * N
+
+F32 = mybir.dt.float32
+BF16 = mybir.dt.bfloat16
+I32 = mybir.dt.int32
+U32 = mybir.dt.uint32
+U16 = mybir.dt.uint16
+U8 = mybir.dt.uint8
+FP8X4 = mybir.dt.float8_e4m3fn_x4
+MULT = mybir.AluOpType.mult
+ADD = mybir.AluOpType.add
+
+P = 128
+PASSES = K // 512
+HALVES = N // P
+LOADS = [[(0, T)]] * (PASSES - 2) + [[(0, 512), (512, 512)]] * 2
+CHUNKS = [[(0, 512, 320), (512, 512, 320)]] * PASSES
+PLANES = [(0, 0), (0, 4), (0, 8), (1, 0), (1, 4)]
+
+
+def tile_moe_res_lin_none_kernel(tc, xT, xr, w_words, w_scales, gate, offs, out):
+    nc = tc.nc
+    with ExitStack() as ctx:
+        lists = ctx.enter_context(tc.tile_pool(name="lists", bufs=1))
+        held = ctx.enter_context(tc.tile_pool(name="held", bufs=1))
+        psum = ctx.enter_context(tc.psum_pool(name="psum", bufs=1))
+
+        offsets = lists.tile([P, SLOTS // 16], U16, name="offsets")
+
+        raw, grouped, words, scales, slot_words, slot_scales = [], [], [], [], [], []
+        for a in range(PASSES):
+            raw.append([held.tile([P, 4, width], F32, name=f"raw{a}_{c0}") for c0, width in LOADS[a]])
+            grouped.append(held.tile([P, T, 4], BF16, name=f"grouped{a}", align_bytes=64))
+            words.append(held.tile([P, T], U32, name=f"words{a}", align_bytes=64))
+            slot_words.append(held.tile([P, SLOTS], U32, name=f"slot_words{a}", align_bytes=64))
+        w_codes = held.tile([P, E * PASSES, N], U32, name="w_codes", align_bytes=64)
+        w_bytes = held.tile([P, E * PASSES, N], U8, name="w_bytes", align_bytes=64)
+        for g in range(2):
+            scales.append(held.tile([P, T], U8, name=f"scales{g}", align_bytes=64))
+            slot_scales.append(held.tile([P, SLOTS], U8, name=f"slot_scales{g}", align_bytes=64))
+        gates = held.tile([P, SLOTS], F32, name="gates")
+        residual, placed, result = [], [], []
+        for h in range(HALVES):
+            residual.append(held.tile([P, T], F32, name=f"residual{h}"))
+            placed.append(held.tile([P, T], F32, name=f"placed{h}"))
+            result.append(held.tile([P, T], F32, name=f"result{h}"))
+
+        w_rows = w_scales.rearrange("e a (q r) n -> q r (e a) n", r=4)
+        for g in range(2):
+            nc.gpsimd.memset(scales[g][:].bitcast(I32), 0)
+        nc.vector.memset(w_bytes[:].bitcast(I32), 0)
+        for h in range(HALVES):
+            nc.gpsimd.memset(placed[h][:], 0.0)
+
+        for a in range(PASSES):
+            for (c0, width), tile in zip(LOADS[a], raw[a]):
+                nc.sync.dma_start(
+                    tile[:],
+                    xT[512 * a : 512 * (a + 1), c0 : c0 + width].rearrange("(p j) w -> p j w", j=4),
+                )
+            if a == 0:
+                nc.sync.dma_start(offsets[:], offs)
+        for q in range(4):
+            nc.sync.dma_start(w_bytes[32 * q : 32 * q + 4, :, :].bitcast(I32), w_rows[q].bitcast(I32))
+        for e in range(E):
+            if e == 1:
+                nc.sync.dma_start(gates[:], gate[0:P, :])
+            for a0, a1 in ((0, 3), (3, PASSES)):
+                nc.sync.dma_start(
+                    w_codes[:, PASSES * e + a0 : PASSES * e + a1, :].bitcast(I32),
+                    w_words[e, a0:a1].rearrange("a p n r -> p a (n r)").bitcast(I32),
+                )
+        for h in range(HALVES):
+            nc.sync.dma_start(residual[h][:], xr[P * h : P * (h + 1), :])
+
+        def cast(copy, a, c0, width):
+            for (first, loaded), tile in zip(LOADS[a], raw[a]):
+                if width and first <= c0 < first + loaded:
+                    copy(
+                        grouped[a][:, c0 : c0 + width, :].rearrange("p (c i) t -> p c t i", i=4),
+                        tile[:, :, c0 - first : c0 - first + width].rearrange("p t (c i) -> p c t i", i=4),
+                    )
+
+        def quantise(a, c0, width):
+            nc.vector.quantize_mx(
+                out=words[a][:, c0 : c0 + width].bitcast(FP8X4),
+                scales=scales[PLANES[a][0]][PLANES[a][1] : P, c0 : c0 + width],
+                in_=grouped[a][:, c0 : c0 + width, :].rearrange("p c t -> p (c t)"),
+            )
+
+        def gather(target, table, s0, s1):
+            columns = offsets[:, s0 // 16 : s1 // 16] if s1 - s0 < SLOTS else offsets[:]
+            nc.vector.tensor_copy(target[:, s0:s1], table[:].indirect(columns))
+
+        steps = [(a, *chunk) for a in range(PASSES) for chunk in CHUNKS[a]]
+        for n in range(len(steps) + 1):
+            if n < len(steps):
+                a, c0, width, share = steps[n]
+                cast(nc.scalar.copy, a, c0, share)
+                cast(nc.vector.tensor_copy, a, c0 + share, width - share)
+            if n > 0:
+                a, c0, width, share = steps[n - 1]
+                quantise(a, c0, width)
+                if c0 == 0 and a > 0:
+                    gather(slot_words[a - 1], words[a - 1], 0, SLOTS)
+                    if a == 3:
+                        gather(slot_scales[0], scales[0], 0, SLOTS)
+        for s in (0, SLOTS // 2):
+            gather(slot_words[PASSES - 1], words[PASSES - 1], s, s + SLOTS // 2)
+            gather(slot_scales[1], scales[1], s, s + SLOTS // 2)
+
+        sums = []
+        for e in range(E):
+            sums.append([])
+            for h in range(HALVES):
+                sums[e].append(psum.tile([P, C], F32, name=f"sum{e}{h}"))
+
+        def multiply(e, passes):
+            for h in range(HALVES):
+                for a in passes:
+                    nc.tensor.matmul_mx(
+                        out=sums[e][h][:],
+                        lhsT=w_codes[:, PASSES * e + a, P * h : P * (h + 1)].bitcast(FP8X4),
+                        lhsT_scale=w_bytes[:, PASSES * e + a, P * h : P * (h + 1)],
+                        rhs=slot_words[a][:, C * e : C * (e + 1)].bitcast(FP8X4),
+                        rhs_scale=slot_scales[PLANES[a][0]][PLANES[a][1] : P, C * e : C * (e + 1)],
+                        start=(a == 0),
+                        stop=(a == PASSES - 1),
+                    )
+
+        product = {}
+
+        def weigh(e):
+            for h in range(HALVES):
+                product[e, h] = held.tile([P, C], F32, name=f"product{e}{h}")
+                nc.scalar.copy(product[e, h][:], sums[e][h][:])
+
+        def place(e, h):
+            nc.vector.tensor_tensor(placed[h][:].indirect(offsets[:, 8 * e : 8 * e + 8]), product[e, h][:], gates[:, C * e : C * (e + 1)], MULT)
+
+        for e in range(E):
+            multiply(e, range(3))
+            if e == 0:
+                multiply(e, [3])
+                multiply(e, [4])
+            else:
+                multiply(e, range(3, PASSES))
+
+        def finish(h, c0, c1):
+            nc.vector.tensor_tensor(result[h][:, c0:c1], placed[h][:, c0:c1], residual[h][:, c0:c1], ADD)
+            nc.sync.dma_start(out[P * h : P * (h + 1), c0:c1], result[h][:, c0:c1])
+
+        for e in range(E):
+            weigh(e)
+        for e in range(E - 2):
+            place(e, 0)
+            place(e, 1)
+        place(2, 0)
+        place(3, 0)
+        place(2, 1)
+        finish(0, 0, T // 2)
+        place(3, 1)
+        finish(0, T // 2, T)
+        finish(1, 0, T // 2)
+        finish(1, T // 2, T)

@@ -1,6 +1,7 @@
 from contextlib import ExitStack
 
 import concourse.mybir as mybir
+from concourse.masks import make_identity
 
 K, T, E, C, N = 2560, 1024, 4, 128, 256
 SLOTS = E * C
@@ -19,9 +20,10 @@ ADD = mybir.AluOpType.add
 P = 128
 PASSES = K // 512
 HALVES = N // P
-LOADS = [[(0, T)]] * (PASSES - 2) + [[(0, 512), (512, 512)]] * 2
-CHUNKS = [[(0, 512, 320), (512, 512, 320)]] * PASSES
-PLANES = [(0, 0), (0, 4), (0, 8), (1, 0), (1, 4)]
+LOADS = [[(0, T)]] * (PASSES - 2) + [[(0, 512), (512, 512)], [(0, 512), (512, 256), (768, 256)]]
+CHUNKS = [[(0, 512, 336), (512, 512, 336)]] * (PASSES - 1) + [[(0, 512, 336), (512, 256, 160), (768, 256, 96)]]
+PLANES = [(0, 0), (0, 4), (1, 4), (1, 8), (1, 0)]
+W_ROWS = (0, 8)
 
 
 def tile_moe_res_lin_none_kernel(tc, xT, xr, w_words, w_scales, gate, offs, out):
@@ -40,11 +42,13 @@ def tile_moe_res_lin_none_kernel(tc, xT, xr, w_words, w_scales, gate, offs, out)
             words.append(held.tile([P, T], U32, name=f"words{a}", align_bytes=64))
             slot_words.append(held.tile([P, SLOTS], U32, name=f"slot_words{a}", align_bytes=64))
         w_codes = held.tile([P, E * PASSES, N], U32, name="w_codes", align_bytes=64)
-        w_bytes = held.tile([P, E * PASSES, N], U8, name="w_bytes", align_bytes=64)
+        w_bytes = [held.tile([P, 2 * PASSES, N], U8, name=f"w_bytes{g}", align_bytes=64) for g in range(2)]
         for g in range(2):
             scales.append(held.tile([P, T], U8, name=f"scales{g}", align_bytes=64))
             slot_scales.append(held.tile([P, SLOTS], U8, name=f"slot_scales{g}", align_bytes=64))
         gates = held.tile([P, SLOTS], F32, name="gates")
+        gate_row = held.tile([P, 4], F32, name="gate_row")
+        identity = held.tile([P, P], F32, name="identity")
         residual, placed, result = [], [], []
         for h in range(HALVES):
             residual.append(held.tile([P, T], F32, name=f"residual{h}"))
@@ -54,7 +58,8 @@ def tile_moe_res_lin_none_kernel(tc, xT, xr, w_words, w_scales, gate, offs, out)
         w_rows = w_scales.rearrange("e a (q r) n -> q r (e a) n", r=4)
         for g in range(2):
             nc.gpsimd.memset(scales[g][:].bitcast(I32), 0)
-        nc.vector.memset(w_bytes[:].bitcast(I32), 0)
+            nc.vector.memset(w_bytes[g][:].bitcast(I32), 0)
+        make_identity(nc, identity[:])
         for h in range(HALVES):
             nc.gpsimd.memset(placed[h][:], 0.0)
 
@@ -66,11 +71,15 @@ def tile_moe_res_lin_none_kernel(tc, xT, xr, w_words, w_scales, gate, offs, out)
                 )
             if a == 0:
                 nc.sync.dma_start(offsets[:], offs)
-        for q in range(4):
-            nc.sync.dma_start(w_bytes[32 * q : 32 * q + 4, :, :].bitcast(I32), w_rows[q].bitcast(I32))
+                nc.sync.dma_start(gate_row[:], gate[0:1, :].rearrange("o (p i) -> (o p) i", i=4))
         for e in range(E):
-            if e == 1:
-                nc.sync.dma_start(gates[:], gate[0:P, :])
+            if e % 2 == 0:
+                for q in range(4):
+                    row = 32 * q + W_ROWS[e // 2]
+                    nc.sync.dma_start(
+                        w_bytes[e // 2][row : row + 4, :, :].bitcast(I32),
+                        w_rows[q][:, PASSES * e : PASSES * (e + 2), :].bitcast(I32),
+                    )
             for a0, a1 in ((0, 3), (3, PASSES)):
                 nc.sync.dma_start(
                     w_codes[:, PASSES * e + a0 : PASSES * e + a1, :].bitcast(I32),
@@ -78,6 +87,11 @@ def tile_moe_res_lin_none_kernel(tc, xT, xr, w_words, w_scales, gate, offs, out)
                 )
         for h in range(HALVES):
             nc.sync.dma_start(residual[h][:], xr[P * h : P * (h + 1), :])
+
+        spread = psum.tile([P, 4, P], F32, name="spread", tag="last")
+        for i in range(4):
+            nc.tensor.transpose(spread[:, i, :], gate_row[:, i : i + 1].to_broadcast([P, P]), identity[:])
+        nc.scalar.copy(gates[:].rearrange("m (p i) -> m p i", i=4), spread[:].rearrange("m i p -> m p i"))
 
         def cast(copy, a, c0, width):
             for (first, loaded), tile in zip(LOADS[a], raw[a]):
@@ -106,11 +120,11 @@ def tile_moe_res_lin_none_kernel(tc, xT, xr, w_words, w_scales, gate, offs, out)
                 cast(nc.vector.tensor_copy, a, c0 + share, width - share)
             if n > 0:
                 a, c0, width, share = steps[n - 1]
-                quantise(a, c0, width)
                 if c0 == 0 and a > 0:
                     gather(slot_words[a - 1], words[a - 1], 0, SLOTS)
-                    if a == 3:
+                    if a == 2:
                         gather(slot_scales[0], scales[0], 0, SLOTS)
+                quantise(a, c0, width)
         for s in (0, SLOTS // 2):
             gather(slot_words[PASSES - 1], words[PASSES - 1], s, s + SLOTS // 2)
             gather(slot_scales[1], scales[1], s, s + SLOTS // 2)
@@ -119,7 +133,7 @@ def tile_moe_res_lin_none_kernel(tc, xT, xr, w_words, w_scales, gate, offs, out)
         for e in range(E):
             sums.append([])
             for h in range(HALVES):
-                sums[e].append(psum.tile([P, C], F32, name=f"sum{e}{h}"))
+                sums[e].append(psum.tile([P, C], F32, name=f"sum{e}{h}", tag="last" if (e, h) == (E - 1, HALVES - 1) else f"sum{e}{h}"))
 
         def multiply(e, passes):
             for h in range(HALVES):
@@ -127,7 +141,7 @@ def tile_moe_res_lin_none_kernel(tc, xT, xr, w_words, w_scales, gate, offs, out)
                     nc.tensor.matmul_mx(
                         out=sums[e][h][:],
                         lhsT=w_codes[:, PASSES * e + a, P * h : P * (h + 1)].bitcast(FP8X4),
-                        lhsT_scale=w_bytes[:, PASSES * e + a, P * h : P * (h + 1)],
+                        lhsT_scale=w_bytes[e // 2][W_ROWS[e // 2] : P, PASSES * (e % 2) + a, P * h : P * (h + 1)],
                         rhs=slot_words[a][:, C * e : C * (e + 1)].bitcast(FP8X4),
                         rhs_scale=slot_scales[PLANES[a][0]][PLANES[a][1] : P, C * e : C * (e + 1)],
                         start=(a == 0),
@@ -145,12 +159,8 @@ def tile_moe_res_lin_none_kernel(tc, xT, xr, w_words, w_scales, gate, offs, out)
             nc.vector.tensor_tensor(placed[h][:].indirect(offsets[:, 8 * e : 8 * e + 8]), product[e, h][:], gates[:, C * e : C * (e + 1)], MULT)
 
         for e in range(E):
-            multiply(e, range(3))
-            if e == 0:
-                multiply(e, [3])
-                multiply(e, [4])
-            else:
-                multiply(e, range(3, PASSES))
+            multiply(e, range(2))
+            multiply(e, range(2, PASSES))
 
         def finish(h, c0, c1):
             nc.vector.tensor_tensor(result[h][:, c0:c1], placed[h][:, c0:c1], residual[h][:, c0:c1], ADD)

@@ -55,7 +55,7 @@ def tile_moe_res_lin_none_kernel(tc, xT, xr, w_words, w_scales, gate, offs, out)
             placed.append(held.tile([P, T], F32, name=f"placed{h}"))
             result.append(held.tile([P, T], F32, name=f"result{h}"))
 
-        w_rows = w_scales.rearrange("e a (q r) n -> q r (e a) n", r=4)
+        w_rows = w_scales.rearrange("e a (q r) n -> r q (e a) n", r=4)
         for g in range(2):
             nc.gpsimd.memset(scales[g][:].bitcast(I32), 0)
             nc.vector.memset(w_bytes[g][:].bitcast(I32), 0)
@@ -74,11 +74,10 @@ def tile_moe_res_lin_none_kernel(tc, xT, xr, w_words, w_scales, gate, offs, out)
                 nc.sync.dma_start(gate_row[:], gate[0:1, :].rearrange("o (p i) -> (o p) i", i=4))
         for e in range(E):
             if e % 2 == 0:
-                for q in range(4):
-                    row = 32 * q + W_ROWS[e // 2]
+                for r in range(4):
                     nc.sync.dma_start(
-                        w_bytes[e // 2][row : row + 4, :, :].bitcast(I32),
-                        w_rows[q][:, PASSES * e : PASSES * (e + 2), :].bitcast(I32),
+                        w_bytes[e // 2][W_ROWS[e // 2] + r : P : 32, :, :].bitcast(I32),
+                        w_rows[r][:, PASSES * e : PASSES * (e + 2), :].bitcast(I32),
                     )
             for a0, a1 in ((0, 3), (3, PASSES)):
                 nc.sync.dma_start(

@@ -21,7 +21,7 @@ P = 128
 PASSES = K // 512
 HALVES = N // P
 LOADS = [[(0, T)]] * (PASSES - 2) + [[(0, 512), (512, 512)], [(0, 512), (512, 256), (768, 256)]]
-CHUNKS = [[(0, 512, 336), (512, 512, 336)]] * (PASSES - 1) + [[(0, 512, 336), (512, 256, 160), (768, 256, 96)]]
+CHUNKS = [[(0, 512, 256), (512, 512, 256)]] * 3 + [[(0, 512, 352), (512, 512, 352)], [(0, 512, 352), (512, 256, 176), (768, 256, 128)]]
 PLANES = [(0, 0), (0, 4), (1, 4), (1, 8), (1, 0)]
 W_ROWS = (0, 8)
 
@@ -63,6 +63,7 @@ def tile_moe_res_lin_none_kernel(tc, xT, xr, w_words, w_scales, gate, offs, out)
         for h in range(HALVES):
             nc.gpsimd.memset(placed[h][:], 0.0)
 
+        nc.scalar.dma_start(gate_row[:], gate[0:1, :].rearrange("o (p i) -> (o p) i", i=4))
         for a in range(PASSES):
             for (c0, width), tile in zip(LOADS[a], raw[a]):
                 nc.sync.dma_start(
@@ -71,7 +72,6 @@ def tile_moe_res_lin_none_kernel(tc, xT, xr, w_words, w_scales, gate, offs, out)
                 )
             if a == 0:
                 nc.sync.dma_start(offsets[:], offs)
-                nc.sync.dma_start(gate_row[:], gate[0:1, :].rearrange("o (p i) -> (o p) i", i=4))
         for e in range(E):
             if e % 2 == 0:
                 for r in range(4):
@@ -124,9 +124,9 @@ def tile_moe_res_lin_none_kernel(tc, xT, xr, w_words, w_scales, gate, offs, out)
                     if a == 2:
                         gather(slot_scales[0], scales[0], 0, SLOTS)
                 quantise(a, c0, width)
-        for s in (0, SLOTS // 2):
-            gather(slot_words[PASSES - 1], words[PASSES - 1], s, s + SLOTS // 2)
-            gather(slot_scales[1], scales[1], s, s + SLOTS // 2)
+        for s0, s1 in ((0, C), (C, SLOTS)):
+            gather(slot_scales[1], scales[1], s0, s1)
+            gather(slot_words[PASSES - 1], words[PASSES - 1], s0, s1)
 
         sums = []
         for e in range(E):

@@ -20,8 +20,8 @@ ADD = mybir.AluOpType.add
 P = 128
 PASSES = K // 512
 HALVES = N // P
-LOADS = [[(0, T)]] * (PASSES - 2) + [[(0, 512), (512, 512)], [(0, 512), (512, 256), (768, 256)]]
-CHUNKS = [[(0, 512, 256), (512, 512, 256)]] * 3 + [[(0, 512, 352), (512, 512, 352)], [(0, 512, 352), (512, 256, 176), (768, 256, 128)]]
+LOADS = [[(0, T)]] * (PASSES - 1) + [[(0, 512), (512, 256), (768, 256)]]
+CHUNKS = [[(0, 512, 256), (512, 512, 256)]] * 3 + [[(0, 512, 320), (512, 512, 320)], [(0, 512, 352), (512, 256, 176), (768, 256, 144)]]
 PLANES = [(0, 0), (0, 4), (1, 4), (1, 8), (1, 0)]
 W_ROWS = (0, 8)
 
@@ -167,14 +167,10 @@ def tile_moe_res_lin_none_kernel(tc, xT, xr, w_words, w_scales, gate, offs, out)
 
         for e in range(E):
             weigh(e)
-        for e in range(E - 2):
+        for e in range(E):
             place(e, 0)
             place(e, 1)
-        place(2, 0)
-        place(3, 0)
-        place(2, 1)
         finish(0, 0, T // 2)
-        place(3, 1)
         finish(0, T // 2, T)
         finish(1, 0, T // 2)
         finish(1, T // 2, T)

@@ -20,10 +20,10 @@ ADD = mybir.AluOpType.add
 P = 128
 PASSES = K // 512
 HALVES = N // P
-LOADS = [[(0, T)]] * (PASSES - 1) + [[(0, 512), (512, 256), (768, 256)]]
-CHUNKS = [[(0, 512, 256), (512, 512, 256)]] * 3 + [[(0, 512, 320), (512, 512, 320)], [(0, 512, 352), (512, 256, 176), (768, 256, 144)]]
-PLANES = [(0, 0), (0, 4), (1, 4), (1, 8), (1, 0)]
-W_ROWS = (0, 8)
+LOADS = [[(0, T)]] * (PASSES - 1) + [[(0, 512), (512, 512)]]
+CHUNKS = [[(0, 512, 256), (512, 512, 256)]] * 4 + [[(0, 512, 448), (512, 256, 128), (768, 256, 128)]]
+PLANES = [(0, 0), (1, 4), (1, 8), (1, 12), (1, 0)]
+W_ROWS = (0, 0)
 
 
 def tile_moe_res_lin_none_kernel(tc, xT, xr, w_words, w_scales, gate, offs, out):
@@ -121,7 +121,7 @@ def tile_moe_res_lin_none_kernel(tc, xT, xr, w_words, w_scales, gate, offs, out)
                 a, c0, width, share = steps[n - 1]
                 if c0 == 0 and a > 0:
                     gather(slot_words[a - 1], words[a - 1], 0, SLOTS)
-                    if a == 2:
+                    if a == 1:
                         gather(slot_scales[0], scales[0], 0, SLOTS)
                 quantise(a, c0, width)
         for s0, s1 in ((0, C), (C, SLOTS)):

@@ -20,8 +20,8 @@ ADD = mybir.AluOpType.add
 P = 128
 PASSES = K // 512
 HALVES = N // P
-LOADS = [[(0, T)]] * (PASSES - 1) + [[(0, 512), (512, 512)]]
-CHUNKS = [[(0, 512, 256), (512, 512, 256)]] * 4 + [[(0, 512, 448), (512, 256, 128), (768, 256, 128)]]
+LOADS = [[(0, T)]] * (PASSES - 1) + [[(0, 512), (512, 256), (768, 256)]]
+CHUNKS = [[(0, 512, share), (512, 512, share)] for share in (256, 320, 256, 256)] + [[(0, 512, 320), (512, 256, 256), (768, 256, 128)]]
 PLANES = [(0, 0), (1, 4), (1, 8), (1, 12), (1, 0)]
 W_ROWS = (0, 0)
 
@@ -63,7 +63,6 @@ def tile_moe_res_lin_none_kernel(tc, xT, xr, w_words, w_scales, gate, offs, out)
         for h in range(HALVES):
             nc.gpsimd.memset(placed[h][:], 0.0)
 
-        nc.scalar.dma_start(gate_row[:], gate[0:1, :].rearrange("o (p i) -> (o p) i", i=4))
         for a in range(PASSES):
             for (c0, width), tile in zip(LOADS[a], raw[a]):
                 nc.sync.dma_start(
@@ -72,6 +71,7 @@ def tile_moe_res_lin_none_kernel(tc, xT, xr, w_words, w_scales, gate, offs, out)
                 )
             if a == 0:
                 nc.sync.dma_start(offsets[:], offs)
+        nc.sync.dma_start(gate_row[:], gate[0:1, :].rearrange("o (p i) -> (o p) i", i=4))
         for e in range(E):
             if e % 2 == 0:
                 for r in range(4):
@@ -86,11 +86,6 @@ def tile_moe_res_lin_none_kernel(tc, xT, xr, w_words, w_scales, gate, offs, out)
                 )
         for h in range(HALVES):
             nc.sync.dma_start(residual[h][:], xr[P * h : P * (h + 1), :])
-
-        spread = psum.tile([P, 4, P], F32, name="spread", tag="last")
-        for i in range(4):
-            nc.tensor.transpose(spread[:, i, :], gate_row[:, i : i + 1].to_broadcast([P, P]), identity[:])
-        nc.scalar.copy(gates[:].rearrange("m (p i) -> m p i", i=4), spread[:].rearrange("m i p -> m p i"))
 
         def cast(copy, a, c0, width):
             for (first, loaded), tile in zip(LOADS[a], raw[a]):
@@ -127,6 +122,11 @@ def tile_moe_res_lin_none_kernel(tc, xT, xr, w_words, w_scales, gate, offs, out)
         for s0, s1 in ((0, C), (C, SLOTS)):
             gather(slot_scales[1], scales[1], s0, s1)
             gather(slot_words[PASSES - 1], words[PASSES - 1], s0, s1)
+
+        spread = psum.tile([P, 4, P], F32, name="spread", tag="last")
+        for i in range(4):
+            nc.tensor.transpose(spread[:, i, :], gate_row[:, i : i + 1].to_broadcast([P, P]), identity[:])
+        nc.scalar.copy(gates[:].rearrange("m (p i) -> m p i", i=4), spread[:].rearrange("m i p -> m p i"))
 
         sums = []
         for e in range(E):

@@ -20,8 +20,15 @@ ADD = mybir.AluOpType.add
 P = 128
 PASSES = K // 512
 HALVES = N // P
-LOADS = [[(0, T)]] * (PASSES - 1) + [[(0, 512), (512, 256), (768, 256)]]
-CHUNKS = [[(0, 512, share), (512, 512, share)] for share in (256, 320, 256, 256)] + [[(0, 512, 320), (512, 256, 256), (768, 256, 128)]]
+LOADS = [[(0, 4, 0, T)]] * 4 + [[(0, 4, 0, 512), (0, 4, 512, 256), (0, 4, 768, 256)]]
+EVEN = [("S", 0, 0, 256), ("V", 0, 512, 512), ("S", 0, 256, 256), ("Q", 0, 256), ("Q", 512, 512), ("Q", 256, 256)]
+STEPS = [
+    EVEN,
+    [("S", 0, 0, 384), ("V", 0, 384, 384), ("S", 0, 768, 256), ("Q", 0, 512), ("Q", 512, 256), ("Q", 768, 256)],
+    EVEN,
+    EVEN,
+    [("S", 0, 0, 320), ("V", 0, 320, 192), ("S", 1, 512, 256), ("S", 2, 768, 128), ("V", 2, 896, 128), ("Q", 0, 512), ("Q", 512, 256), ("Q", 768, 256)],
+]
 PLANES = [(0, 0), (1, 4), (1, 8), (1, 12), (1, 0)]
 W_ROWS = (0, 0)
 
@@ -37,7 +44,7 @@ def tile_moe_res_lin_none_kernel(tc, xT, xr, w_words, w_scales, gate, offs, out)
 
         raw, grouped, words, scales, slot_words, slot_scales = [], [], [], [], [], []
         for a in range(PASSES):
-            raw.append([held.tile([P, 4, width], F32, name=f"raw{a}_{c0}") for c0, width in LOADS[a]])
+            raw.append([held.tile([P, rows, width], F32, name=f"raw{a}_{j0}_{c0}") for j0, rows, c0, width in LOADS[a]])
             grouped.append(held.tile([P, T, 4], BF16, name=f"grouped{a}", align_bytes=64))
             words.append(held.tile([P, T], U32, name=f"words{a}", align_bytes=64))
             slot_words.append(held.tile([P, SLOTS], U32, name=f"slot_words{a}", align_bytes=64))
@@ -64,10 +71,10 @@ def tile_moe_res_lin_none_kernel(tc, xT, xr, w_words, w_scales, gate, offs, out)
             nc.gpsimd.memset(placed[h][:], 0.0)
 
         for a in range(PASSES):
-            for (c0, width), tile in zip(LOADS[a], raw[a]):
+            for (j0, rows, c0, width), tile in zip(LOADS[a], raw[a]):
                 nc.sync.dma_start(
                     tile[:],
-                    xT[512 * a : 512 * (a + 1), c0 : c0 + width].rearrange("(p j) w -> p j w", j=4),
+                    xT[512 * a : 512 * (a + 1), c0 : c0 + width].rearrange("(p j) w -> p j w", j=4)[:, j0 : j0 + rows, :],
                 )
             if a == 0:
                 nc.sync.dma_start(offsets[:], offs)
@@ -87,13 +94,12 @@ def tile_moe_res_lin_none_kernel(tc, xT, xr, w_words, w_scales, gate, offs, out)
         for h in range(HALVES):
             nc.sync.dma_start(residual[h][:], xr[P * h : P * (h + 1), :])
 
-        def cast(copy, a, c0, width):
-            for (first, loaded), tile in zip(LOADS[a], raw[a]):
-                if width and first <= c0 < first + loaded:
-                    copy(
-                        grouped[a][:, c0 : c0 + width, :].rearrange("p (c i) t -> p c t i", i=4),
-                        tile[:, :, c0 - first : c0 - first + width].rearrange("p t (c i) -> p c t i", i=4),
-                    )
+        def cast(copy, a, load, c0, width):
+            j0, rows, first, loaded = LOADS[a][load]
+            copy(
+                grouped[a][:, c0 : c0 + width, j0 : j0 + rows].rearrange("p (c i) t -> p c t i", i=4),
+                raw[a][load][:, :, c0 - first : c0 - first + width].rearrange("p t (c i) -> p c t i", i=4),
+            )
 
         def quantise(a, c0, width):
             nc.vector.quantize_mx(
@@ -106,19 +112,16 @@ def tile_moe_res_lin_none_kernel(tc, xT, xr, w_words, w_scales, gate, offs, out)
             columns = offsets[:, s0 // 16 : s1 // 16] if s1 - s0 < SLOTS else offsets[:]
             nc.vector.tensor_copy(target[:, s0:s1], table[:].indirect(columns))
 
-        steps = [(a, *chunk) for a in range(PASSES) for chunk in CHUNKS[a]]
-        for n in range(len(steps) + 1):
-            if n < len(steps):
-                a, c0, width, share = steps[n]
-                cast(nc.scalar.copy, a, c0, share)
-                cast(nc.vector.tensor_copy, a, c0 + share, width - share)
-            if n > 0:
-                a, c0, width, share = steps[n - 1]
-                if c0 == 0 and a > 0:
-                    gather(slot_words[a - 1], words[a - 1], 0, SLOTS)
-                    if a == 1:
-                        gather(slot_scales[0], scales[0], 0, SLOTS)
-                quantise(a, c0, width)
+        for a in range(PASSES):
+            for kind, *where in STEPS[a]:
+                if kind == "Q":
+                    quantise(a, *where)
+                else:
+                    cast(nc.scalar.copy if kind == "S" else nc.vector.tensor_copy, a, *where)
+            if a < PASSES - 1:
+                gather(slot_words[a], words[a], 0, SLOTS)
+            if a == 0:
+                gather(slot_scales[0], scales[0], 0, SLOTS)
         for s0, s1 in ((0, C), (C, SLOTS)):
             gather(slot_scales[1], scales[1], s0, s1)
             gather(slot_words[PASSES - 1], words[PASSES - 1], s0, s1)

@@ -16,6 +16,7 @@ U8 = mybir.dt.uint8
 FP8X4 = mybir.dt.float8_e4m3fn_x4
 MULT = mybir.AluOpType.mult
 ADD = mybir.AluOpType.add
+COPY = mybir.ActivationFunctionType.Copy
 
 P = 128
 PASSES = K // 512
@@ -155,10 +156,17 @@ def tile_moe_res_lin_none_kernel(tc, xT, xr, w_words, w_scales, gate, offs, out)
         def weigh(e):
             for h in range(HALVES):
                 product[e, h] = held.tile([P, C], F32, name=f"product{e}{h}")
-                nc.scalar.copy(product[e, h][:], sums[e][h][:])
+                if h == 0:
+                    nc.scalar.copy(product[e, h][:], sums[e][h][:])
+                else:
+                    nc.vector.tensor_tensor(product[e, h][:], sums[e][h][:], gates[:, C * e : C * (e + 1)], MULT)
 
         def place(e, h):
-            nc.vector.tensor_tensor(placed[h][:].indirect(offsets[:, 8 * e : 8 * e + 8]), product[e, h][:], gates[:, C * e : C * (e + 1)], MULT)
+            window = placed[h][:].indirect(offsets[:, 8 * e : 8 * e + 8])
+            if h == 0:
+                nc.vector.tensor_tensor(window, product[e, h][:], gates[:, C * e : C * (e + 1)], MULT)
+            else:
+                nc.scalar.activation(window, product[e, h][:], COPY)
 
         for e in range(E):
             multiply(e, range(2))
@@ -170,7 +178,6 @@ def tile_moe_res_lin_none_kernel(tc, xT, xr, w_words, w_scales, gate, offs, out)
 
         for e in range(E):
             weigh(e)
-        for e in range(E):
             place(e, 0)
             place(e, 1)
         finish(0, 0, T // 2)

@@ -19,19 +19,41 @@ ADD = mybir.AluOpType.add
 COPY = mybir.ActivationFunctionType.Copy
 
 P = 128
-PASSES = K // 512
+PACK = 4
+PASSES = K // (P * PACK)
+LAST = PASSES - 1
 HALVES = N // P
-LOADS = [[(0, 4, 0, T)]] * 4 + [[(0, 4, 0, 512), (0, 4, 512, 256), (0, 4, 768, 256)]]
+PER_COLUMN = 16
+
+LOADS = [[(0, T)]] * LAST + [[(0, 512), (512, 256), (768, 256)]]
 EVEN = [("S", 0, 0, 256), ("V", 0, 512, 512), ("S", 0, 256, 256), ("Q", 0, 256), ("Q", 512, 512), ("Q", 256, 256)]
-STEPS = [
-    EVEN,
-    [("S", 0, 0, 384), ("V", 0, 384, 384), ("S", 0, 768, 256), ("Q", 0, 512), ("Q", 512, 256), ("Q", 768, 256)],
-    EVEN,
-    EVEN,
-    [("S", 0, 0, 320), ("V", 0, 320, 192), ("S", 1, 512, 256), ("S", 2, 768, 128), ("V", 2, 896, 128), ("Q", 0, 512), ("Q", 512, 256), ("Q", 768, 256)],
+SECOND = [("S", 0, 0, 384), ("V", 0, 384, 384), ("S", 0, 768, 256), ("Q", 0, 512), ("Q", 512, 256), ("Q", 768, 256)]
+FINAL = [
+    ("S", 0, 0, 320),
+    ("V", 0, 320, 192),
+    ("S", 1, 512, 256),
+    ("S", 2, 768, 128),
+    ("V", 2, 896, 128),
+    ("Q", 0, 512),
+    ("Q", 512, 256),
+    ("Q", 896, 128),
+    ("Q", 768, 128),
 ]
+FOURTH = [
+    ("S", 0, 0, 256),
+    ("V", 0, 512, 512),
+    ("S", 0, 256, 128),
+    ("S", 0, 384, 128),
+    ("Q", 0, 256),
+    ("Q", 512, 512),
+    ("Q", 256, 128),
+    ("Q", 384, 128),
+]
+STEPS = [EVEN, SECOND, EVEN, FOURTH, FINAL]
 PLANES = [(0, 0), (1, 4), (1, 8), (1, 12), (1, 0)]
-W_ROWS = (0, 0)
+GROUPS = ((0, 2), (2, 3), (3, E))
+W_LOADS = ((0, 3), (3, PASSES))
+OPENING = 2
 
 
 def tile_moe_res_lin_none_kernel(tc, xT, xr, w_words, w_scales, gate, offs, out):
@@ -41,21 +63,21 @@ def tile_moe_res_lin_none_kernel(tc, xT, xr, w_words, w_scales, gate, offs, out)
         held = ctx.enter_context(tc.tile_pool(name="held", bufs=1))
         psum = ctx.enter_context(tc.psum_pool(name="psum", bufs=1))
 
-        offsets = lists.tile([P, SLOTS // 16], U16, name="offsets")
+        offsets = lists.tile([P, SLOTS // PER_COLUMN], U16, name="offsets")
 
         raw, grouped, words, scales, slot_words, slot_scales = [], [], [], [], [], []
         for a in range(PASSES):
-            raw.append([held.tile([P, rows, width], F32, name=f"raw{a}_{j0}_{c0}") for j0, rows, c0, width in LOADS[a]])
-            grouped.append(held.tile([P, T, 4], BF16, name=f"grouped{a}", align_bytes=64))
+            raw.append([held.tile([P, PACK, width], F32, name=f"raw{a}_{c0}") for c0, width in LOADS[a]])
+            grouped.append(held.tile([P, T, PACK], BF16, name=f"grouped{a}", align_bytes=64))
             words.append(held.tile([P, T], U32, name=f"words{a}", align_bytes=64))
             slot_words.append(held.tile([P, SLOTS], U32, name=f"slot_words{a}", align_bytes=64))
         w_codes = held.tile([P, E * PASSES, N], U32, name="w_codes", align_bytes=64)
-        w_bytes = [held.tile([P, 2 * PASSES, N], U8, name=f"w_bytes{g}", align_bytes=64) for g in range(2)]
+        w_bytes = [held.tile([P, (e1 - e0) * PASSES, N], U8, name=f"w_bytes{e0}", align_bytes=64) for e0, e1 in GROUPS]
         for g in range(2):
             scales.append(held.tile([P, T], U8, name=f"scales{g}", align_bytes=64))
             slot_scales.append(held.tile([P, SLOTS], U8, name=f"slot_scales{g}", align_bytes=64))
         gates = held.tile([P, SLOTS], F32, name="gates")
-        gate_row = held.tile([P, 4], F32, name="gate_row")
+        gate_row = held.tile([P, SLOTS // P], F32, name="gate_row")
         identity = held.tile([P, P], F32, name="identity")
         residual, placed, result = [], [], []
         for h in range(HALVES):
@@ -63,55 +85,59 @@ def tile_moe_res_lin_none_kernel(tc, xT, xr, w_words, w_scales, gate, offs, out)
             placed.append(held.tile([P, T], F32, name=f"placed{h}"))
             result.append(held.tile([P, T], F32, name=f"result{h}"))
 
-        w_rows = w_scales.rearrange("e a (q r) n -> r q (e a) n", r=4)
-        for g in range(2):
-            nc.gpsimd.memset(scales[g][:].bitcast(I32), 0)
-            nc.vector.memset(w_bytes[g][:].bitcast(I32), 0)
+        for tile in scales:
+            nc.gpsimd.memset(tile[:].bitcast(I32), 0)
+        for tile in w_bytes:
+            nc.vector.memset(tile[:].bitcast(I32), 0)
         make_identity(nc, identity[:])
         for h in range(HALVES):
             nc.gpsimd.memset(placed[h][:], 0.0)
 
         for a in range(PASSES):
-            for (j0, rows, c0, width), tile in zip(LOADS[a], raw[a]):
-                nc.sync.dma_start(
-                    tile[:],
-                    xT[512 * a : 512 * (a + 1), c0 : c0 + width].rearrange("(p j) w -> p j w", j=4)[:, j0 : j0 + rows, :],
-                )
+            for (c0, width), tile in zip(LOADS[a], raw[a]):
+                rows = xT[P * PACK * a : P * PACK * (a + 1), c0 : c0 + width]
+                nc.sync.dma_start(tile[:], rows.rearrange("(p t) w -> p t w", t=PACK))
             if a == 0:
                 nc.sync.dma_start(offsets[:], offs)
-        nc.sync.dma_start(gate_row[:], gate[0:1, :].rearrange("o (p i) -> (o p) i", i=4))
-        for e in range(E):
-            if e % 2 == 0:
-                for r in range(4):
-                    nc.sync.dma_start(
-                        w_bytes[e // 2][W_ROWS[e // 2] + r : P : 32, :, :].bitcast(I32),
-                        w_rows[r][:, PASSES * e : PASSES * (e + 2), :].bitcast(I32),
-                    )
-            for a0, a1 in ((0, 3), (3, PASSES)):
+        nc.sync.dma_start(gate_row[:], gate[0:1, :].rearrange("o (p i) -> (o p) i", p=P))
+        w_rows = w_scales.rearrange("e a (q r) n -> r q (e a) n", r=4)
+        w_scale = {}
+        for tile, (e0, e1) in zip(w_bytes, GROUPS):
+            for r in range(4):
                 nc.sync.dma_start(
-                    w_codes[:, PASSES * e + a0 : PASSES * e + a1, :].bitcast(I32),
-                    w_words[e, a0:a1].rearrange("a p n r -> p a (n r)").bitcast(I32),
+                    tile[r:P:32, :, :].bitcast(I32),
+                    w_rows[r][:, PASSES * e0 : PASSES * e1, :].bitcast(I32),
                 )
+            for e in range(e0, e1):
+                w_scale[e] = tile[:, PASSES * (e - e0) : PASSES * (e - e0 + 1), :]
+                for a0, a1 in W_LOADS:
+                    nc.sync.dma_start(
+                        w_codes[:, PASSES * e + a0 : PASSES * e + a1, :].bitcast(I32),
+                        w_words[e, a0:a1].rearrange("a p n r -> p a (n r)").bitcast(I32),
+                    )
         for h in range(HALVES):
             nc.sync.dma_start(residual[h][:], xr[P * h : P * (h + 1), :])
 
         def cast(copy, a, load, c0, width):
-            j0, rows, first, loaded = LOADS[a][load]
+            first = LOADS[a][load][0]
             copy(
-                grouped[a][:, c0 : c0 + width, j0 : j0 + rows].rearrange("p (c i) t -> p c t i", i=4),
+                grouped[a][:, c0 : c0 + width, :].rearrange("p (c i) t -> p c t i", i=4),
                 raw[a][load][:, :, c0 - first : c0 - first + width].rearrange("p t (c i) -> p c t i", i=4),
             )
 
         def quantise(a, c0, width):
+            tile, row = PLANES[a]
             nc.vector.quantize_mx(
                 out=words[a][:, c0 : c0 + width].bitcast(FP8X4),
-                scales=scales[PLANES[a][0]][PLANES[a][1] : P, c0 : c0 + width],
+                scales=scales[tile][row:P, c0 : c0 + width],
                 in_=grouped[a][:, c0 : c0 + width, :].rearrange("p c t -> p (c t)"),
             )
 
+        def entries(s0, s1):
+            return offsets[:, s0 // PER_COLUMN : s1 // PER_COLUMN]
+
         def gather(target, table, s0, s1):
-            columns = offsets[:, s0 // 16 : s1 // 16] if s1 - s0 < SLOTS else offsets[:]
-            nc.vector.tensor_copy(target[:, s0:s1], table[:].indirect(columns))
+            nc.vector.tensor_copy(target[:, s0:s1], table[:].indirect(entries(s0, s1)))
 
         for a in range(PASSES):
             for kind, *where in STEPS[a]:
@@ -119,68 +145,60 @@ def tile_moe_res_lin_none_kernel(tc, xT, xr, w_words, w_scales, gate, offs, out)
                     quantise(a, *where)
                 else:
                     cast(nc.scalar.copy if kind == "S" else nc.vector.tensor_copy, a, *where)
-            if a < PASSES - 1:
+            if a < LAST:
                 gather(slot_words[a], words[a], 0, SLOTS)
             if a == 0:
                 gather(slot_scales[0], scales[0], 0, SLOTS)
         for s0, s1 in ((0, C), (C, SLOTS)):
             gather(slot_scales[1], scales[1], s0, s1)
-            gather(slot_words[PASSES - 1], words[PASSES - 1], s0, s1)
+            gather(slot_words[LAST], words[LAST], s0, s1)
 
-        spread = psum.tile([P, 4, P], F32, name="spread", tag="last")
-        for i in range(4):
+        spread = psum.tile([P, SLOTS // P, P], F32, name="spread", tag="last")
+        for i in range(SLOTS // P):
             nc.tensor.transpose(spread[:, i, :], gate_row[:, i : i + 1].to_broadcast([P, P]), identity[:])
-        nc.scalar.copy(gates[:].rearrange("m (p i) -> m p i", i=4), spread[:].rearrange("m i p -> m p i"))
+        nc.scalar.copy(gates[:].rearrange("m (p i) -> m p i", p=P), spread[:].rearrange("m i p -> m p i"))
 
-        sums = []
+        sums = {}
         for e in range(E):
-            sums.append([])
             for h in range(HALVES):
-                sums[e].append(psum.tile([P, C], F32, name=f"sum{e}{h}", tag="last" if (e, h) == (E - 1, HALVES - 1) else f"sum{e}{h}"))
+                tag = "last" if (e, h) == (E - 1, HALVES - 1) else f"sum{e}{h}"
+                sums[e, h] = psum.tile([P, C], F32, name=f"sum{e}{h}", tag=tag)
 
         def multiply(e, passes):
             for h in range(HALVES):
                 for a in passes:
+                    tile, row = PLANES[a]
                     nc.tensor.matmul_mx(
-                        out=sums[e][h][:],
+                        out=sums[e, h][:],
                         lhsT=w_codes[:, PASSES * e + a, P * h : P * (h + 1)].bitcast(FP8X4),
-                        lhsT_scale=w_bytes[e // 2][W_ROWS[e // 2] : P, PASSES * (e % 2) + a, P * h : P * (h + 1)],
+                        lhsT_scale=w_scale[e][:, a, P * h : P * (h + 1)],
                         rhs=slot_words[a][:, C * e : C * (e + 1)].bitcast(FP8X4),
-                        rhs_scale=slot_scales[PLANES[a][0]][PLANES[a][1] : P, C * e : C * (e + 1)],
+                        rhs_scale=slot_scales[tile][row:P, C * e : C * (e + 1)],
                         start=(a == 0),
-                        stop=(a == PASSES - 1),
+                        stop=(a == LAST),
                     )
 
-        product = {}
+        for e in range(E):
+            multiply(e, range(OPENING))
+            multiply(e, range(OPENING, PASSES))
 
-        def weigh(e):
+        for e in range(E):
+            weight = gates[:, C * e : C * (e + 1)]
+            product = []
             for h in range(HALVES):
-                product[e, h] = held.tile([P, C], F32, name=f"product{e}{h}")
-                if h == 0:
-                    nc.scalar.copy(product[e, h][:], sums[e][h][:])
+                product.append(held.tile([P, C], F32, name=f"product{e}{h}"))
+                if (e, h) == (E - 1, HALVES - 1):
+                    nc.vector.tensor_tensor(product[h][:], sums[e, h][:], weight, MULT)
                 else:
-                    nc.vector.tensor_tensor(product[e, h][:], sums[e][h][:], gates[:, C * e : C * (e + 1)], MULT)
+                    nc.scalar.copy(product[h][:], sums[e, h][:])
+            for h in range(HALVES):
+                window = placed[h][:].indirect(entries(C * e, C * (e + 1)))
+                if (e, h) == (E - 1, HALVES - 1):
+                    nc.scalar.activation(window, product[h][:], COPY)
+                else:
+                    nc.vector.tensor_tensor(window, product[h][:], weight, MULT)
 
-        def place(e, h):
-            window = placed[h][:].indirect(offsets[:, 8 * e : 8 * e + 8])
-            if h == 0:
-                nc.vector.tensor_tensor(window, product[e, h][:], gates[:, C * e : C * (e + 1)], MULT)
-            else:
-                nc.scalar.activation(window, product[e, h][:], COPY)
-
-        for e in range(E):
-            multiply(e, range(2))
-            multiply(e, range(2, PASSES))
-
-        def finish(h, c0, c1):
-            nc.vector.tensor_tensor(result[h][:, c0:c1], placed[h][:, c0:c1], residual[h][:, c0:c1], ADD)
-            nc.sync.dma_start(out[P * h : P * (h + 1), c0:c1], result[h][:, c0:c1])
-
-        for e in range(E):
-            weigh(e)
-            place(e, 0)
-            place(e, 1)
-        finish(0, 0, T // 2)
-        finish(0, T // 2, T)
-        finish(1, 0, T // 2)
-        finish(1, T // 2, T)
+        for h in range(HALVES):
+            for c0, c1 in ((0, T // 2), (T // 2, T)):
+                nc.vector.tensor_tensor(result[h][:, c0:c1], placed[h][:, c0:c1], residual[h][:, c0:c1], ADD)
+                nc.sync.dma_start(out[P * h : P * (h + 1), c0:c1], result[h][:, c0:c1])

@@ -24,36 +24,51 @@ PASSES = K // (P * PACK)
 LAST = PASSES - 1
 HALVES = N // P
 PER_COLUMN = 16
+QUADRANT = 32
+QUADRANTS = P // QUADRANT
+SCALE_ROWS = 4
+ROW_WORDS = N // 4
 
-LOADS = [[(0, T)]] * LAST + [[(0, 512), (512, 256), (768, 256)]]
-EVEN = [("S", 0, 0, 256), ("V", 0, 512, 512), ("S", 0, 256, 256), ("Q", 0, 256), ("Q", 512, 512), ("Q", 256, 256)]
-SECOND = [("S", 0, 0, 384), ("V", 0, 384, 384), ("S", 0, 768, 256), ("Q", 0, 512), ("Q", 512, 256), ("Q", 768, 256)]
-FINAL = [
-    ("S", 0, 0, 320),
-    ("V", 0, 320, 192),
-    ("S", 1, 512, 256),
-    ("S", 2, 768, 128),
-    ("V", 2, 896, 128),
+LOADS = [[(0, 2), (2, 4)]] * 3 + [[(0, 2), (2, 3), (3, 4)]] * 2
+STEADY = [
+    ("G", "S", 0, 0, 512),
+    ("G", "S", 1, 0, 256),
+    ("G", "V", 1, 256, 512),
+    ("G", "V", 2, 0, 512),
+    ("G", "S", 3, 0, 512),
+    ("W", "V", 0, 512),
     ("Q", 0, 512),
-    ("Q", 512, 256),
-    ("Q", 896, 128),
-    ("Q", 768, 128),
 ]
 FOURTH = [
-    ("S", 0, 0, 256),
-    ("V", 0, 512, 512),
-    ("S", 0, 256, 128),
-    ("S", 0, 384, 128),
-    ("Q", 0, 256),
-    ("Q", 512, 512),
-    ("Q", 256, 128),
-    ("Q", 384, 128),
+    ("G", "S", 0, 0, 512),
+    ("G", "S", 1, 0, 512),
+    ("G", "V", 2, 0, 512),
+    ("G", "V", 3, 0, 256),
+    ("G", "S", 3, 256, 512),
+    ("W", "V", 0, 512),
+    ("Q", 0, 512),
 ]
-STEPS = [EVEN, SECOND, EVEN, FOURTH, FINAL]
-PLANES = [(0, 0), (1, 4), (1, 8), (1, 12), (1, 0)]
-GROUPS = ((0, 2), (2, 3), (3, E))
+FINAL = [
+    ("G", "S", 0, 0, 256),
+    ("G", "S", 1, 0, 256),
+    ("G", "S", 0, 256, 512),
+    ("G", "V", 1, 256, 512),
+    ("G", "V", 2, 0, 256),
+    ("G", "S", 2, 256, 512),
+    ("G", "V", 3, 0, 256),
+    ("G", "V", 3, 256, 384),
+    ("G", "S", 3, 384, 512),
+    ("W", "V", 0, 128),
+    ("W", "V", 128, 256),
+    ("Q", 0, 128),
+    ("Q", 128, 256),
+    ("W", "S", 384, 512),
+    ("W", "V", 256, 384),
+    ("Q", 256, 512),
+]
+STEPS = [STEADY, STEADY, STEADY, FOURTH, FINAL]
+ON_SCALAR = ((0, 1), (1, 1), (2, 1), (3, 1))
 W_LOADS = ((0, 3), (3, PASSES))
-OPENING = 2
 
 
 def tile_moe_res_lin_none_kernel(tc, xT, xr, w_words, w_scales, gate, offs, out):
@@ -64,18 +79,9 @@ def tile_moe_res_lin_none_kernel(tc, xT, xr, w_words, w_scales, gate, offs, out)
         psum = ctx.enter_context(tc.psum_pool(name="psum", bufs=1))
 
         offsets = lists.tile([P, SLOTS // PER_COLUMN], U16, name="offsets")
-
-        raw, grouped, words, scales, slot_words, slot_scales = [], [], [], [], [], []
-        for a in range(PASSES):
-            raw.append([held.tile([P, PACK, width], F32, name=f"raw{a}_{c0}") for c0, width in LOADS[a]])
-            grouped.append(held.tile([P, T, PACK], BF16, name=f"grouped{a}", align_bytes=64))
-            words.append(held.tile([P, T], U32, name=f"words{a}", align_bytes=64))
-            slot_words.append(held.tile([P, SLOTS], U32, name=f"slot_words{a}", align_bytes=64))
+        staged = held.tile([P, PASSES, QUADRANTS, N], U8, name="staged")
+        w_bytes = held.tile([P, QUADRANTS, PASSES * N], U8, name="w_bytes", align_bytes=64)
         w_codes = held.tile([P, E * PASSES, N], U32, name="w_codes", align_bytes=64)
-        w_bytes = [held.tile([P, (e1 - e0) * PASSES, N], U8, name=f"w_bytes{e0}", align_bytes=64) for e0, e1 in GROUPS]
-        for g in range(2):
-            scales.append(held.tile([P, T], U8, name=f"scales{g}", align_bytes=64))
-            slot_scales.append(held.tile([P, SLOTS], U8, name=f"slot_scales{g}", align_bytes=64))
         gates = held.tile([P, SLOTS], F32, name="gates")
         gate_row = held.tile([P, SLOTS // P], F32, name="gate_row")
         identity = held.tile([P, P], F32, name="identity")
@@ -85,78 +91,97 @@ def tile_moe_res_lin_none_kernel(tc, xT, xr, w_words, w_scales, gate, offs, out)
             placed.append(held.tile([P, T], F32, name=f"placed{h}"))
             result.append(held.tile([P, T], F32, name=f"result{h}"))
 
-        for tile in scales:
-            nc.gpsimd.memset(tile[:].bitcast(I32), 0)
-        for tile in w_bytes:
-            nc.vector.memset(tile[:].bitcast(I32), 0)
+        nc.vector.memset(w_bytes[:, 0, :].bitcast(I32), 0)
+        nc.vector.memset(w_bytes[0:QUADRANT, QUADRANTS - 1, :].bitcast(I32), 0)
+        nc.gpsimd.memset(placed[0][:], 0.0)
+        nc.scalar.copy(placed[1][:], placed[0][:])
         make_identity(nc, identity[:])
-        for h in range(HALVES):
-            nc.gpsimd.memset(placed[h][:], 0.0)
 
+        w_rows = w_scales.rearrange("e a (q r) n -> r e (a q) n", r=SCALE_ROWS)
+        for r in range(SCALE_ROWS):
+            nc.sync.dma_start(
+                staged[r : SCALE_ROWS * E : SCALE_ROWS].rearrange("p a q n -> p (a q) n").bitcast(I32),
+                w_rows[r].bitcast(I32),
+            )
+        row = {}
         for a in range(PASSES):
-            for (c0, width), tile in zip(LOADS[a], raw[a]):
-                rows = xT[P * PACK * a : P * PACK * (a + 1), c0 : c0 + width]
-                nc.sync.dma_start(tile[:], rows.rearrange("(p t) w -> p t w", t=PACK))
+            rows = xT[P * PACK * a : P * PACK * (a + 1), :].rearrange("(p t) w -> p t w", t=PACK)
+            for t0, t1 in LOADS[a]:
+                raw = held.tile([P, t1 - t0, T], F32, name=f"raw{a}_{t0}")
+                nc.sync.dma_start(raw[:], rows[:, t0:t1, :])
+                for t in range(t0, t1):
+                    row[a, t] = raw[:, t - t0, :]
+                if (a, t0) == (0, 0):
+                    nc.sync.dma_start(offsets[:], offs)
             if a == 0:
-                nc.sync.dma_start(offsets[:], offs)
-        nc.sync.dma_start(gate_row[:], gate[0:1, :].rearrange("o (p i) -> (o p) i", p=P))
-        w_rows = w_scales.rearrange("e a (q r) n -> r q (e a) n", r=4)
-        w_scale = {}
-        for tile, (e0, e1) in zip(w_bytes, GROUPS):
-            for r in range(4):
+                nc.sync.dma_start(gate_row[:], gate[0:1, :].rearrange("o (p i) -> (o p) i", p=P))
+        for e in range(E):
+            for a0, a1 in W_LOADS:
                 nc.sync.dma_start(
-                    tile[r:P:32, :, :].bitcast(I32),
-                    w_rows[r][:, PASSES * e0 : PASSES * e1, :].bitcast(I32),
+                    w_codes[:, PASSES * e + a0 : PASSES * e + a1, :].bitcast(I32),
+                    w_words[e, a0:a1].rearrange("a p n r -> p a (n r)").bitcast(I32),
                 )
-            for e in range(e0, e1):
-                w_scale[e] = tile[:, PASSES * (e - e0) : PASSES * (e - e0 + 1), :]
-                for a0, a1 in W_LOADS:
-                    nc.sync.dma_start(
-                        w_codes[:, PASSES * e + a0 : PASSES * e + a1, :].bitcast(I32),
-                        w_words[e, a0:a1].rearrange("a p n r -> p a (n r)").bitcast(I32),
-                    )
         for h in range(HALVES):
             nc.sync.dma_start(residual[h][:], xr[P * h : P * (h + 1), :])
 
-        def cast(copy, a, load, c0, width):
-            first = LOADS[a][load][0]
-            copy(
-                grouped[a][:, c0 : c0 + width, :].rearrange("p (c i) t -> p c t i", i=4),
-                raw[a][load][:, :, c0 - first : c0 - first + width].rearrange("p t (c i) -> p c t i", i=4),
+        live = SCALE_ROWS * E
+        nc.vector.tensor_copy(
+            w_bytes[0:live].bitcast(I32).rearrange("p q (a n) -> p q a n", a=PASSES),
+            staged[0:live].bitcast(I32).rearrange("p a q n -> p q a n"),
+        )
+        for q in range(1, QUADRANTS):
+            count = QUADRANT if q == QUADRANTS - 1 else live
+            nc.vector.tensor_copy(
+                w_bytes[QUADRANT * q : QUADRANT * q + count, 0, :].bitcast(I32),
+                w_bytes[0:count, q, :].bitcast(I32),
             )
-
-        def quantise(a, c0, width):
-            tile, row = PLANES[a]
-            nc.vector.quantize_mx(
-                out=words[a][:, c0 : c0 + width].bitcast(FP8X4),
-                scales=scales[tile][row:P, c0 : c0 + width],
-                in_=grouped[a][:, c0 : c0 + width, :].rearrange("p c t -> p (c t)"),
-            )
-
-        def entries(s0, s1):
-            return offsets[:, s0 // PER_COLUMN : s1 // PER_COLUMN]
-
-        def gather(target, table, s0, s1):
-            nc.vector.tensor_copy(target[:, s0:s1], table[:].indirect(entries(s0, s1)))
-
-        for a in range(PASSES):
-            for kind, *where in STEPS[a]:
-                if kind == "Q":
-                    quantise(a, *where)
-                else:
-                    cast(nc.scalar.copy if kind == "S" else nc.vector.tensor_copy, a, *where)
-            if a < LAST:
-                gather(slot_words[a], words[a], 0, SLOTS)
-            if a == 0:
-                gather(slot_scales[0], scales[0], 0, SLOTS)
-        for s0, s1 in ((0, C), (C, SLOTS)):
-            gather(slot_scales[1], scales[1], s0, s1)
-            gather(slot_words[LAST], words[LAST], s0, s1)
 
         spread = psum.tile([P, SLOTS // P, P], F32, name="spread", tag="last")
         for i in range(SLOTS // P):
             nc.tensor.transpose(spread[:, i, :], gate_row[:, i : i + 1].to_broadcast([P, P]), identity[:])
         nc.scalar.copy(gates[:].rearrange("m (p i) -> m p i", p=P), spread[:].rearrange("m i p -> m p i"))
+
+        def entries(s0, s1):
+            return offsets[:, s0 // PER_COLUMN : s1 // PER_COLUMN]
+
+        slot_words, slot_scales = {}, {}
+        for a in range(PASSES):
+            parts = [(0, SLOTS)] if a < LAST else [(0, SLOTS // 2), (SLOTS // 2, SLOTS)]
+            picked = {s0: held.tile([P, PACK, s1 - s0], F32, name=f"picked{a}_{s0}") for s0, s1 in parts}
+            woven = {
+                s0: held.tile([P, s1 - s0, PACK], BF16, name=f"woven{a}_{s0}", align_bytes=64) for s0, s1 in parts
+            }
+            for kind, *where in STEPS[a]:
+                if kind == "G":
+                    engine, t, s0, s1 = where
+                    base = max(b for b in picked if b <= s0)
+                    target = picked[base][:, t, s0 - base : s1 - base]
+                    window = row[a, t].indirect(entries(s0, s1))
+                    if engine == "S":
+                        nc.scalar.activation(target, window, COPY)
+                    else:
+                        nc.vector.tensor_copy(target, window)
+                elif kind == "W":
+                    engine, s0, s1 = where
+                    copy = nc.scalar.copy if engine == "S" else nc.vector.tensor_copy
+                    base = max(b for b in picked if b <= s0)
+                    copy(
+                        woven[base][:, s0 - base : s1 - base, :].rearrange("p (c i) t -> p c t i", i=4),
+                        picked[base][:, :, s0 - base : s1 - base].rearrange("p t (c i) -> p c t i", i=4),
+                    )
+                else:
+                    s0, s1 = where
+                    words = held.tile([P, s1 - s0], U32, name=f"words{a}_{s0}", align_bytes=64)
+                    scales = held.tile([P, s1 - s0], U8, name=f"scales{a}_{s0}", align_bytes=64)
+                    base = max(b for b in picked if b <= s0)
+                    nc.vector.quantize_mx(
+                        out=words[:].bitcast(FP8X4),
+                        scales=scales[:],
+                        in_=woven[base][:, s0 - base : s1 - base, :].rearrange("p c t -> p (c t)"),
+                    )
+                    for e in range(s0 // C, s1 // C):
+                        slot_words[a, e] = words[:, C * e - s0 : C * (e + 1) - s0]
+                        slot_scales[a, e] = scales[:, C * e - s0 : C * (e + 1) - s0]
 
         sums = {}
         for e in range(E):
@@ -164,36 +189,32 @@ def tile_moe_res_lin_none_kernel(tc, xT, xr, w_words, w_scales, gate, offs, out)
                 tag = "last" if (e, h) == (E - 1, HALVES - 1) else f"sum{e}{h}"
                 sums[e, h] = psum.tile([P, C], F32, name=f"sum{e}{h}", tag=tag)
 
-        def multiply(e, passes):
-            for h in range(HALVES):
-                for a in passes:
-                    tile, row = PLANES[a]
-                    nc.tensor.matmul_mx(
-                        out=sums[e, h][:],
-                        lhsT=w_codes[:, PASSES * e + a, P * h : P * (h + 1)].bitcast(FP8X4),
-                        lhsT_scale=w_scale[e][:, a, P * h : P * (h + 1)],
-                        rhs=slot_words[a][:, C * e : C * (e + 1)].bitcast(FP8X4),
-                        rhs_scale=slot_scales[tile][row:P, C * e : C * (e + 1)],
-                        start=(a == 0),
-                        stop=(a == LAST),
-                    )
-
         for e in range(E):
-            multiply(e, range(OPENING))
-            multiply(e, range(OPENING, PASSES))
+            for a0, a1 in W_LOADS:
+                for h in range(HALVES):
+                    for a in range(a0, a1):
+                        nc.tensor.matmul_mx(
+                            out=sums[e, h][:],
+                            lhsT=w_codes[:, PASSES * e + a, P * h : P * (h + 1)].bitcast(FP8X4),
+                            lhsT_scale=w_bytes[SCALE_ROWS * e : P, 0, N * a + P * h : N * a + P * (h + 1)],
+                            rhs=slot_words[a, e].bitcast(FP8X4),
+                            rhs_scale=slot_scales[a, e],
+                            start=(a == 0),
+                            stop=(a == LAST),
+                        )
 
         for e in range(E):
             weight = gates[:, C * e : C * (e + 1)]
             product = []
             for h in range(HALVES):
                 product.append(held.tile([P, C], F32, name=f"product{e}{h}"))
-                if (e, h) == (E - 1, HALVES - 1):
+                if (e, h) in ON_SCALAR:
                     nc.vector.tensor_tensor(product[h][:], sums[e, h][:], weight, MULT)
                 else:
                     nc.scalar.copy(product[h][:], sums[e, h][:])
             for h in range(HALVES):
                 window = placed[h][:].indirect(entries(C * e, C * (e + 1)))
-                if (e, h) == (E - 1, HALVES - 1):
+                if (e, h) in ON_SCALAR:
                     nc.scalar.activation(window, product[h][:], COPY)
                 else:
                     nc.vector.tensor_tensor(window, product[h][:], weight, MULT)

@@ -25,11 +25,9 @@ LAST = PASSES - 1
 HALVES = N // P
 PER_COLUMN = 16
 QUADRANT = 32
-QUADRANTS = P // QUADRANT
 SCALE_ROWS = 4
-ROW_WORDS = N // 4
 
-LOADS = [[(0, 2), (2, 4)]] * 3 + [[(0, 2), (2, 3), (3, 4)]] * 2
+LOADS = [[(0, 2), (2, 4)]] * 4 + [[(0, 2), (2, 3), (3, 4)]]
 STEADY = [
     ("G", "S", 0, 0, 512),
     ("G", "S", 1, 0, 256),
@@ -39,20 +37,11 @@ STEADY = [
     ("W", "V", 0, 512),
     ("Q", 0, 512),
 ]
-FOURTH = [
-    ("G", "S", 0, 0, 512),
-    ("G", "S", 1, 0, 512),
-    ("G", "V", 2, 0, 512),
-    ("G", "V", 3, 0, 256),
-    ("G", "S", 3, 256, 512),
-    ("W", "V", 0, 512),
-    ("Q", 0, 512),
-]
 FINAL = [
     ("G", "S", 0, 0, 256),
     ("G", "S", 1, 0, 256),
     ("G", "S", 0, 256, 512),
-    ("G", "V", 1, 256, 512),
+    ("G", "S", 1, 256, 512),
     ("G", "V", 2, 0, 256),
     ("G", "S", 2, 256, 512),
     ("G", "V", 3, 0, 256),
@@ -66,8 +55,9 @@ FINAL = [
     ("W", "V", 256, 384),
     ("Q", 256, 512),
 ]
-STEPS = [STEADY, STEADY, STEADY, FOURTH, FINAL]
-ON_SCALAR = ((0, 1), (1, 1), (2, 1), (3, 1))
+STEPS = [STEADY, STEADY, STEADY, STEADY, FINAL]
+ON_SCALAR = ((1, 1), (3, 1))
+GROUPS = ((0, 1), (1, 2), (2, 3), (3, E))
 W_LOADS = ((0, 3), (3, PASSES))
 
 
@@ -79,8 +69,7 @@ def tile_moe_res_lin_none_kernel(tc, xT, xr, w_words, w_scales, gate, offs, out)
         psum = ctx.enter_context(tc.psum_pool(name="psum", bufs=1))
 
         offsets = lists.tile([P, SLOTS // PER_COLUMN], U16, name="offsets")
-        staged = held.tile([P, PASSES, QUADRANTS, N], U8, name="staged")
-        w_bytes = held.tile([P, QUADRANTS, PASSES * N], U8, name="w_bytes", align_bytes=64)
+        w_bytes = [held.tile([P, (e1 - e0) * PASSES, N], U8, name=f"w_bytes{e0}", align_bytes=64) for e0, e1 in GROUPS]
         w_codes = held.tile([P, E * PASSES, N], U32, name="w_codes", align_bytes=64)
         gates = held.tile([P, SLOTS], F32, name="gates")
         gate_row = held.tile([P, SLOTS // P], F32, name="gate_row")
@@ -91,18 +80,12 @@ def tile_moe_res_lin_none_kernel(tc, xT, xr, w_words, w_scales, gate, offs, out)
             placed.append(held.tile([P, T], F32, name=f"placed{h}"))
             result.append(held.tile([P, T], F32, name=f"result{h}"))
 
-        nc.vector.memset(w_bytes[:, 0, :].bitcast(I32), 0)
-        nc.vector.memset(w_bytes[0:QUADRANT, QUADRANTS - 1, :].bitcast(I32), 0)
+        for tile in w_bytes:
+            nc.vector.memset(tile[:].bitcast(I32), 0)
         nc.gpsimd.memset(placed[0][:], 0.0)
         nc.scalar.copy(placed[1][:], placed[0][:])
         make_identity(nc, identity[:])
 
-        w_rows = w_scales.rearrange("e a (q r) n -> r e (a q) n", r=SCALE_ROWS)
-        for r in range(SCALE_ROWS):
-            nc.sync.dma_start(
-                staged[r : SCALE_ROWS * E : SCALE_ROWS].rearrange("p a q n -> p (a q) n").bitcast(I32),
-                w_rows[r].bitcast(I32),
-            )
         row = {}
         for a in range(PASSES):
             rows = xT[P * PACK * a : P * PACK * (a + 1), :].rearrange("(p t) w -> p t w", t=PACK)
@@ -115,26 +98,23 @@ def tile_moe_res_lin_none_kernel(tc, xT, xr, w_words, w_scales, gate, offs, out)
                     nc.sync.dma_start(offsets[:], offs)
             if a == 0:
                 nc.sync.dma_start(gate_row[:], gate[0:1, :].rearrange("o (p i) -> (o p) i", p=P))
-        for e in range(E):
-            for a0, a1 in W_LOADS:
+        w_rows = w_scales.rearrange("e a (q r) n -> r q (e a) n", r=SCALE_ROWS)
+        w_scale = {}
+        for tile, (e0, e1) in zip(w_bytes, GROUPS):
+            for r in range(SCALE_ROWS):
                 nc.sync.dma_start(
-                    w_codes[:, PASSES * e + a0 : PASSES * e + a1, :].bitcast(I32),
-                    w_words[e, a0:a1].rearrange("a p n r -> p a (n r)").bitcast(I32),
+                    tile[r:P:QUADRANT, :, :].bitcast(I32),
+                    w_rows[r][:, PASSES * e0 : PASSES * e1, :].bitcast(I32),
                 )
+            for e in range(e0, e1):
+                w_scale[e] = tile[:, PASSES * (e - e0) : PASSES * (e - e0 + 1), :]
+                for a0, a1 in W_LOADS:
+                    nc.sync.dma_start(
+                        w_codes[:, PASSES * e + a0 : PASSES * e + a1, :].bitcast(I32),
+                        w_words[e, a0:a1].rearrange("a p n r -> p a (n r)").bitcast(I32),
+                    )
         for h in range(HALVES):
             nc.sync.dma_start(residual[h][:], xr[P * h : P * (h + 1), :])
-
-        live = SCALE_ROWS * E
-        nc.vector.tensor_copy(
-            w_bytes[0:live].bitcast(I32).rearrange("p q (a n) -> p q a n", a=PASSES),
-            staged[0:live].bitcast(I32).rearrange("p a q n -> p q a n"),
-        )
-        for q in range(1, QUADRANTS):
-            count = QUADRANT if q == QUADRANTS - 1 else live
-            nc.vector.tensor_copy(
-                w_bytes[QUADRANT * q : QUADRANT * q + count, 0, :].bitcast(I32),
-                w_bytes[0:count, q, :].bitcast(I32),
-            )
 
         spread = psum.tile([P, SLOTS // P, P], F32, name="spread", tag="last")
         for i in range(SLOTS // P):
@@ -196,7 +176,7 @@ def tile_moe_res_lin_none_kernel(tc, xT, xr, w_words, w_scales, gate, offs, out)
                         nc.tensor.matmul_mx(
                             out=sums[e, h][:],
                             lhsT=w_codes[:, PASSES * e + a, P * h : P * (h + 1)].bitcast(FP8X4),
-                            lhsT_scale=w_bytes[SCALE_ROWS * e : P, 0, N * a + P * h : N * a + P * (h + 1)],
+                            lhsT_scale=w_scale[e][:, a, P * h : P * (h + 1)],
                             rhs=slot_words[a, e].bitcast(FP8X4),
                             rhs_scale=slot_scales[a, e],
                             start=(a == 0),

@@ -56,9 +56,8 @@ FINAL = [
     ("Q", 256, 512),
 ]
 STEPS = [STEADY, STEADY, STEADY, STEADY, FINAL]
-ON_SCALAR = ((1, 1), (3, 1))
+ON_SCALAR = ((0, 1), (1, 1), (2, 1), (3, 1))
 GROUPS = ((0, 1), (1, 2), (2, 3), (3, E))
-W_LOADS = ((0, 3), (3, PASSES))
 
 
 def tile_moe_res_lin_none_kernel(tc, xT, xr, w_words, w_scales, gate, offs, out):
@@ -71,14 +70,13 @@ def tile_moe_res_lin_none_kernel(tc, xT, xr, w_words, w_scales, gate, offs, out)
         offsets = lists.tile([P, SLOTS // PER_COLUMN], U16, name="offsets")
         w_bytes = [held.tile([P, (e1 - e0) * PASSES, N], U8, name=f"w_bytes{e0}", align_bytes=64) for e0, e1 in GROUPS]
         w_codes = held.tile([P, E * PASSES, N], U32, name="w_codes", align_bytes=64)
-        gates = held.tile([P, SLOTS], F32, name="gates")
+        gates = held.tile([P, SLOTS], F32, name="gates", tag="gates")
         gate_row = held.tile([P, SLOTS // P], F32, name="gate_row")
         identity = held.tile([P, P], F32, name="identity")
-        residual, placed, result = [], [], []
+        residual, placed = [], []
         for h in range(HALVES):
             residual.append(held.tile([P, T], F32, name=f"residual{h}"))
             placed.append(held.tile([P, T], F32, name=f"placed{h}"))
-            result.append(held.tile([P, T], F32, name=f"result{h}"))
 
         for tile in w_bytes:
             nc.vector.memset(tile[:].bitcast(I32), 0)
@@ -99,6 +97,7 @@ def tile_moe_res_lin_none_kernel(tc, xT, xr, w_words, w_scales, gate, offs, out)
             if a == 0:
                 nc.sync.dma_start(gate_row[:], gate[0:1, :].rearrange("o (p i) -> (o p) i", p=P))
         w_rows = w_scales.rearrange("e a (q r) n -> r q (e a) n", r=SCALE_ROWS)
+        w_loads = [[(0, 3, 0, N), (3, PASSES, 0, N)]] * (E - 1) + [[(0, PASSES, 0, P), (0, PASSES, P, N)]]
         w_scale = {}
         for tile, (e0, e1) in zip(w_bytes, GROUPS):
             for r in range(SCALE_ROWS):
@@ -108,10 +107,10 @@ def tile_moe_res_lin_none_kernel(tc, xT, xr, w_words, w_scales, gate, offs, out)
                 )
             for e in range(e0, e1):
                 w_scale[e] = tile[:, PASSES * (e - e0) : PASSES * (e - e0 + 1), :]
-                for a0, a1 in W_LOADS:
+                for a0, a1, n0, n1 in w_loads[e]:
                     nc.sync.dma_start(
-                        w_codes[:, PASSES * e + a0 : PASSES * e + a1, :].bitcast(I32),
-                        w_words[e, a0:a1].rearrange("a p n r -> p a (n r)").bitcast(I32),
+                        w_codes[:, PASSES * e + a0 : PASSES * e + a1, n0:n1].bitcast(I32),
+                        w_words[e, a0:a1, :, n0:n1].rearrange("a p n r -> p a (n r)").bitcast(I32),
                     )
         for h in range(HALVES):
             nc.sync.dma_start(residual[h][:], xr[P * h : P * (h + 1), :])
@@ -170,8 +169,8 @@ def tile_moe_res_lin_none_kernel(tc, xT, xr, w_words, w_scales, gate, offs, out)
                 sums[e, h] = psum.tile([P, C], F32, name=f"sum{e}{h}", tag=tag)
 
         for e in range(E):
-            for a0, a1 in W_LOADS:
-                for h in range(HALVES):
+            for a0, a1, n0, n1 in w_loads[e]:
+                for h in range(n0 // P, n1 // P):
                     for a in range(a0, a1):
                         nc.tensor.matmul_mx(
                             out=sums[e, h][:],
@@ -201,5 +200,7 @@ def tile_moe_res_lin_none_kernel(tc, xT, xr, w_words, w_scales, gate, offs, out)
 
         for h in range(HALVES):
             for c0, c1 in ((0, T // 2), (T // 2, T)):
-                nc.vector.tensor_tensor(result[h][:, c0:c1], placed[h][:, c0:c1], residual[h][:, c0:c1], ADD)
-                nc.sync.dma_start(out[P * h : P * (h + 1), c0:c1], result[h][:, c0:c1])
+                tag = "gates" if (h, c0) == (0, 0) else f"result{h}_{c0}"
+                result = held.tile([P, c1 - c0], F32, name=f"result{h}_{c0}", tag=tag)
+                nc.vector.tensor_tensor(result[:], placed[h][:, c0:c1], residual[h][:, c0:c1], ADD)
+                nc.sync.dma_start(out[P * h : P * (h + 1), c0:c1], result[:])

@@ -56,8 +56,7 @@ FINAL = [
     ("Q", 256, 512),
 ]
 STEPS = [STEADY, STEADY, STEADY, STEADY, FINAL]
-ON_SCALAR = ((0, 1), (1, 1), (2, 1), (3, 1))
-GROUPS = ((0, 1), (1, 2), (2, 3), (3, E))
+GROUPS = ((0, 2), (2, E))
 
 
 def tile_moe_res_lin_none_kernel(tc, xT, xr, w_words, w_scales, gate, offs, out):
@@ -99,19 +98,21 @@ def tile_moe_res_lin_none_kernel(tc, xT, xr, w_words, w_scales, gate, offs, out)
         w_rows = w_scales.rearrange("e a (q r) n -> r q (e a) n", r=SCALE_ROWS)
         w_loads = [[(0, 3, 0, N), (3, PASSES, 0, N)]] * (E - 1) + [[(0, PASSES, 0, P), (0, PASSES, P, N)]]
         w_scale = {}
-        for tile, (e0, e1) in zip(w_bytes, GROUPS):
-            for r in range(SCALE_ROWS):
-                nc.sync.dma_start(
-                    tile[r:P:QUADRANT, :, :].bitcast(I32),
-                    w_rows[r][:, PASSES * e0 : PASSES * e1, :].bitcast(I32),
-                )
-            for e in range(e0, e1):
-                w_scale[e] = tile[:, PASSES * (e - e0) : PASSES * (e - e0 + 1), :]
-                for a0, a1, n0, n1 in w_loads[e]:
+        for e in range(E):
+            if e < len(GROUPS):
+                e0, e1 = GROUPS[e]
+                for r in range(SCALE_ROWS):
                     nc.sync.dma_start(
-                        w_codes[:, PASSES * e + a0 : PASSES * e + a1, n0:n1].bitcast(I32),
-                        w_words[e, a0:a1, :, n0:n1].rearrange("a p n r -> p a (n r)").bitcast(I32),
+                        w_bytes[e][r:P:QUADRANT, :, :].bitcast(I32),
+                        w_rows[r][:, PASSES * e0 : PASSES * e1, :].bitcast(I32),
                     )
+                for member in range(e0, e1):
+                    w_scale[member] = w_bytes[e][:, PASSES * (member - e0) : PASSES * (member - e0 + 1), :]
+            for a0, a1, n0, n1 in w_loads[e]:
+                nc.sync.dma_start(
+                    w_codes[:, PASSES * e + a0 : PASSES * e + a1, n0:n1].bitcast(I32),
+                    w_words[e, a0:a1, :, n0:n1].rearrange("a p n r -> p a (n r)").bitcast(I32),
+                )
         for h in range(HALVES):
             nc.sync.dma_start(residual[h][:], xr[P * h : P * (h + 1), :])
 
@@ -183,20 +184,12 @@ def tile_moe_res_lin_none_kernel(tc, xT, xr, w_words, w_scales, gate, offs, out)
                         )
 
         for e in range(E):
-            weight = gates[:, C * e : C * (e + 1)]
             product = []
             for h in range(HALVES):
                 product.append(held.tile([P, C], F32, name=f"product{e}{h}"))
-                if (e, h) in ON_SCALAR:
-                    nc.vector.tensor_tensor(product[h][:], sums[e, h][:], weight, MULT)
-                else:
-                    nc.scalar.copy(product[h][:], sums[e, h][:])
-            for h in range(HALVES):
-                window = placed[h][:].indirect(entries(C * e, C * (e + 1)))
-                if (e, h) in ON_SCALAR:
-                    nc.scalar.activation(window, product[h][:], COPY)
-                else:
-                    nc.vector.tensor_tensor(window, product[h][:], weight, MULT)
+                nc.vector.tensor_tensor(product[h][:], sums[e, h][:], gates[:, C * e : C * (e + 1)], MULT)
+            nc.vector.tensor_copy(placed[0][:].indirect(entries(C * e, C * (e + 1))), product[0][:])
+            nc.scalar.activation(placed[1][:].indirect(entries(C * e, C * (e + 1))), product[1][:], COPY)
 
         for h in range(HALVES):
             for c0, c1 in ((0, T // 2), (T // 2, T)):

@@ -96,7 +96,7 @@ def tile_moe_res_lin_none_kernel(tc, xT, xr, w_words, w_scales, gate, offs, out)
             if a == 0:
                 nc.sync.dma_start(gate_row[:], gate[0:1, :].rearrange("o (p i) -> (o p) i", p=P))
         w_rows = w_scales.rearrange("e a (q r) n -> r q (e a) n", r=SCALE_ROWS)
-        w_loads = [[(0, 3, 0, N), (3, PASSES, 0, N)]] * (E - 1) + [[(0, PASSES, 0, P), (0, PASSES, P, N)]]
+        w_loads = [[(0, 3, 0, N), (3, PASSES, 0, N)]] * 2 + [[(0, 3, 0, N), (3, 4, 0, N), (4, PASSES, 0, N)]] * 2
         w_scale = {}
         for e in range(E):
             if e < len(GROUPS):

@@ -25,7 +25,13 @@ LAST = PASSES - 1
 HALVES = N // P
 PER_COLUMN = 16
 QUADRANT = 32
+QUADRANTS = P // QUADRANT
 SCALE_ROWS = 4
+PLANES = 4
+GROUP_ROWS = PLANES * SCALE_ROWS
+SPREAD = 16
+LANDING = QUADRANT
+FREE_ROWS = 4
 
 LOADS = [[(0, 2), (2, 4)]] * 4 + [[(0, 2), (2, 3), (3, 4)]]
 STEADY = [
@@ -56,7 +62,6 @@ FINAL = [
     ("Q", 256, 512),
 ]
 STEPS = [STEADY, STEADY, STEADY, STEADY, FINAL]
-GROUPS = ((0, 2), (2, E))
 
 
 def tile_moe_res_lin_none_kernel(tc, xT, xr, w_words, w_scales, gate, offs, out):
@@ -67,59 +72,70 @@ def tile_moe_res_lin_none_kernel(tc, xT, xr, w_words, w_scales, gate, offs, out)
         psum = ctx.enter_context(tc.psum_pool(name="psum", bufs=1))
 
         offsets = lists.tile([P, SLOTS // PER_COLUMN], U16, name="offsets")
-        w_bytes = [held.tile([P, (e1 - e0) * PASSES, N], U8, name=f"w_bytes{e0}", align_bytes=64) for e0, e1 in GROUPS]
-        w_codes = held.tile([P, E * PASSES, N], U32, name="w_codes", align_bytes=64)
+        landed = held.tile([P, QUADRANTS, N], U8, name="landed", align_bytes=64)
+        lowered = held.tile([P, 2, QUADRANTS, N], U8, name="lowered", align_bytes=64)
+        dealt = [held.tile([P, N], U8, name=f"dealt{g}", align_bytes=64) for g in range(SPREAD // PLANES)]
         gates = held.tile([P, SLOTS], F32, name="gates", tag="gates")
-        gate_row = held.tile([P, SLOTS // P], F32, name="gate_row")
+        gate_row = held.tile([P, SLOTS // P], F32, name="gate_row", tag="gate_row", align_bytes=64)
         identity = held.tile([P, P], F32, name="identity")
-        residual, placed = [], []
-        for h in range(HALVES):
-            residual.append(held.tile([P, T], F32, name=f"residual{h}"))
-            placed.append(held.tile([P, T], F32, name=f"placed{h}"))
+        placed = [held.tile([P, T], F32, name=f"placed{h}") for h in range(HALVES)]
 
-        for tile in w_bytes:
-            nc.vector.memset(tile[:].bitcast(I32), 0)
+        nc.sync.dma_start(gate_row[:], gate[0:1, :].rearrange("o (p i) -> (o p) i", p=P))
+        top = P - QUADRANT
+        nc.vector.memset(lowered[top:P].bitcast(I32), 0)
+        by_row = w_scales.rearrange("e a (q r) n -> r (e a) q n", r=SCALE_ROWS)
+        for r in range(SCALE_ROWS):
+            queue = nc.scalar if r < SCALE_ROWS // 2 else nc.sync
+            queue.dma_start(
+                landed[LANDING + r : LANDING + SCALE_ROWS * SPREAD : SCALE_ROWS].bitcast(I32),
+                by_row[r][0:SPREAD].bitcast(I32),
+            )
+        source = {}
+        for g in range(SPREAD // PLANES):
+            first = LANDING + GROUP_ROWS * g
+            if first % QUADRANT == 0:
+                source[g] = landed[first : first + QUADRANT]
+            else:
+                nc.sync.dma_start(
+                    lowered[top : top + GROUP_ROWS, g // 2].rearrange("p q n -> p (q n)").bitcast(I32),
+                    landed[first : first + GROUP_ROWS].rearrange("p q n -> p (q n)").bitcast(I32),
+                )
+                source[g] = lowered[top:P, g // 2]
+        for g in (0, 2, 1, 3):
+            for q in range(QUADRANTS):
+                nc.vector.tensor_copy(
+                    dealt[g][QUADRANT * q : QUADRANT * (q + 1), :].bitcast(I32), source[g][:, q, :].bitcast(I32)
+                )
+
+        def w_scale(e, a, h):
+            g, j = divmod(PASSES * e + a, PLANES)
+            if g < len(dealt):
+                return dealt[g][SCALE_ROWS * j :, P * h : P * (h + 1)]
+            return direct[:, j, P * h : P * (h + 1)]
+
+        make_identity(nc, identity[:])
         nc.gpsimd.memset(placed[0][:], 0.0)
         nc.scalar.copy(placed[1][:], placed[0][:])
-        make_identity(nc, identity[:])
-
-        row = {}
-        for a in range(PASSES):
-            rows = xT[P * PACK * a : P * PACK * (a + 1), :].rearrange("(p t) w -> p t w", t=PACK)
-            for t0, t1 in LOADS[a]:
-                raw = held.tile([P, t1 - t0, T], F32, name=f"raw{a}_{t0}")
-                nc.sync.dma_start(raw[:], rows[:, t0:t1, :])
-                for t in range(t0, t1):
-                    row[a, t] = raw[:, t - t0, :]
-                if (a, t0) == (0, 0):
-                    nc.sync.dma_start(offsets[:], offs)
-            if a == 0:
-                nc.sync.dma_start(gate_row[:], gate[0:1, :].rearrange("o (p i) -> (o p) i", p=P))
-        w_rows = w_scales.rearrange("e a (q r) n -> r q (e a) n", r=SCALE_ROWS)
-        w_loads = [[(0, 3, 0, N), (3, PASSES, 0, N)]] * 2 + [[(0, 3, 0, N), (3, 4, 0, N), (4, PASSES, 0, N)]] * 2
-        w_scale = {}
-        for e in range(E):
-            if e < len(GROUPS):
-                e0, e1 = GROUPS[e]
-                for r in range(SCALE_ROWS):
-                    nc.sync.dma_start(
-                        w_bytes[e][r:P:QUADRANT, :, :].bitcast(I32),
-                        w_rows[r][:, PASSES * e0 : PASSES * e1, :].bitcast(I32),
-                    )
-                for member in range(e0, e1):
-                    w_scale[member] = w_bytes[e][:, PASSES * (member - e0) : PASSES * (member - e0 + 1), :]
-            for a0, a1, n0, n1 in w_loads[e]:
-                nc.sync.dma_start(
-                    w_codes[:, PASSES * e + a0 : PASSES * e + a1, n0:n1].bitcast(I32),
-                    w_words[e, a0:a1, :, n0:n1].rearrange("a p n r -> p a (n r)").bitcast(I32),
-                )
-        for h in range(HALVES):
-            nc.sync.dma_start(residual[h][:], xr[P * h : P * (h + 1), :])
 
         spread = psum.tile([P, SLOTS // P, P], F32, name="spread", tag="last")
         for i in range(SLOTS // P):
             nc.tensor.transpose(spread[:, i, :], gate_row[:, i : i + 1].to_broadcast([P, P]), identity[:])
         nc.scalar.copy(gates[:].rearrange("m (p i) -> m p i", p=P), spread[:].rearrange("m i p -> m p i"))
+
+        row = {}
+        later = held.tile([P, PACK * PASSES - FREE_ROWS, T], F32, name="later", tag="gate_row", align_bytes=64)
+        for a in range(PASSES):
+            rows = xT[P * PACK * a : P * PACK * (a + 1), :].rearrange("(p t) w -> p t w", t=PACK)
+            for t0, t1 in LOADS[a]:
+                if PACK * a + t0 < FREE_ROWS:
+                    raw = held.tile([P, t1 - t0, T], F32, name=f"raw{a}_{t0}")[:]
+                else:
+                    raw = later[:, PACK * a + t0 - FREE_ROWS : PACK * a + t1 - FREE_ROWS, :]
+                nc.sync.dma_start(raw, rows[:, t0:t1, :])
+                for t in range(t0, t1):
+                    row[a, t] = raw[:, t - t0, :]
+                if (a, t0) == (0, 0):
+                    nc.sync.dma_start(offsets[:], offs)
 
         def entries(s0, s1):
             return offsets[:, s0 // PER_COLUMN : s1 // PER_COLUMN]
@@ -127,7 +143,7 @@ def tile_moe_res_lin_none_kernel(tc, xT, xr, w_words, w_scales, gate, offs, out)
         slot_words, slot_scales = {}, {}
         for a in range(PASSES):
             parts = [(0, SLOTS)] if a < LAST else [(0, SLOTS // 2), (SLOTS // 2, SLOTS)]
-            picked = {s0: held.tile([P, PACK, s1 - s0], F32, name=f"picked{a}_{s0}") for s0, s1 in parts}
+            picked = {s0: held.tile([P, PACK, s1 - s0], F32, name=f"picked{a}_{s0}", align_bytes=64) for s0, s1 in parts}
             woven = {
                 s0: held.tile([P, s1 - s0, PACK], BF16, name=f"woven{a}_{s0}", align_bytes=64) for s0, s1 in parts
             }
@@ -163,6 +179,23 @@ def tile_moe_res_lin_none_kernel(tc, xT, xr, w_words, w_scales, gate, offs, out)
                         slot_words[a, e] = words[:, C * e - s0 : C * (e + 1) - s0]
                         slot_scales[a, e] = scales[:, C * e - s0 : C * (e + 1) - s0]
 
+        direct = held.tile([P, E * PASSES - SPREAD, N], U8, name="direct", tag="picked1_0", align_bytes=64)
+        nc.vector.memset(direct[:].bitcast(I32), 0)
+        by_quadrant = w_scales.rearrange("e a (q r) n -> r q (e a) n", r=SCALE_ROWS)
+        for r in range(SCALE_ROWS):
+            nc.sync.dma_start(direct[r:P:QUADRANT].bitcast(I32), by_quadrant[r][:, SPREAD:, :].bitcast(I32))
+        w_codes = held.tile([P, E * PASSES, N], U32, name="w_codes", tag="picked2_0", align_bytes=64)
+        w_loads = [[(0, 3), (3, PASSES)]] * 2 + [[(0, 3), (3, 4), (4, PASSES)]] * 2
+        for e in range(E):
+            for a0, a1 in w_loads[e]:
+                nc.sync.dma_start(
+                    w_codes[:, PASSES * e + a0 : PASSES * e + a1, :].bitcast(I32),
+                    w_words[e, a0:a1].rearrange("a p n r -> p a (n r)").bitcast(I32),
+                )
+        residual = held.tile([P, HALVES, T], F32, name="residual", tag="picked3_0", align_bytes=64)
+        for h in range(HALVES):
+            nc.sync.dma_start(residual[:, h, :], xr[P * h : P * (h + 1), :])
+
         sums = {}
         for e in range(E):
             for h in range(HALVES):
@@ -170,13 +203,13 @@ def tile_moe_res_lin_none_kernel(tc, xT, xr, w_words, w_scales, gate, offs, out)
                 sums[e, h] = psum.tile([P, C], F32, name=f"sum{e}{h}", tag=tag)
 
         for e in range(E):
-            for a0, a1, n0, n1 in w_loads[e]:
-                for h in range(n0 // P, n1 // P):
+            for a0, a1 in w_loads[e]:
+                for h in range(HALVES):
                     for a in range(a0, a1):
                         nc.tensor.matmul_mx(
                             out=sums[e, h][:],
                             lhsT=w_codes[:, PASSES * e + a, P * h : P * (h + 1)].bitcast(FP8X4),
-                            lhsT_scale=w_scale[e][:, a, P * h : P * (h + 1)],
+                            lhsT_scale=w_scale(e, a, h),
                             rhs=slot_words[a, e].bitcast(FP8X4),
                             rhs_scale=slot_scales[a, e],
                             start=(a == 0),
@@ -195,5 +228,5 @@ def tile_moe_res_lin_none_kernel(tc, xT, xr, w_words, w_scales, gate, offs, out)
             for c0, c1 in ((0, T // 2), (T // 2, T)):
                 tag = "gates" if (h, c0) == (0, 0) else f"result{h}_{c0}"
                 result = held.tile([P, c1 - c0], F32, name=f"result{h}_{c0}", tag=tag)
-                nc.vector.tensor_tensor(result[:], placed[h][:, c0:c1], residual[h][:, c0:c1], ADD)
+                nc.vector.tensor_tensor(result[:], placed[h][:, c0:c1], residual[:, h, c0:c1], ADD)
                 nc.sync.dma_start(out[P * h : P * (h + 1), c0:c1], result[:])

@@ -43,6 +43,14 @@ STEADY = [
     ("W", "V", 0, 512),
     ("Q", 0, 512),
 ]
+OPENING = [
+    ("G", "S", 0, 0, 512),
+    ("G", "S", 1, 0, 512),
+    ("G", "V", 2, 0, 512),
+    ("G", "S", 3, 0, 512),
+    ("W", "V", 0, 512),
+    ("Q", 0, 512),
+]
 FINAL = [
     ("G", "S", 0, 0, 256),
     ("G", "S", 1, 0, 256),
@@ -61,7 +69,7 @@ FINAL = [
     ("W", "V", 256, 384),
     ("Q", 256, 512),
 ]
-STEPS = [STEADY, STEADY, STEADY, STEADY, FINAL]
+STEPS = [OPENING, OPENING, OPENING, OPENING, FINAL]
 
 
 def tile_moe_res_lin_none_kernel(tc, xT, xr, w_words, w_scales, gate, offs, out):
@@ -73,8 +81,7 @@ def tile_moe_res_lin_none_kernel(tc, xT, xr, w_words, w_scales, gate, offs, out)
 
         offsets = lists.tile([P, SLOTS // PER_COLUMN], U16, name="offsets")
         landed = held.tile([P, QUADRANTS, N], U8, name="landed", align_bytes=64)
-        lowered = held.tile([P, 2, QUADRANTS, N], U8, name="lowered", align_bytes=64)
-        dealt = [held.tile([P, N], U8, name=f"dealt{g}", align_bytes=64) for g in range(SPREAD // PLANES)]
+        lowered = held.tile([P, QUADRANTS, 2, N], U8, name="lowered", align_bytes=64)
         gates = held.tile([P, SLOTS], F32, name="gates", tag="gates")
         gate_row = held.tile([P, SLOTS // P], F32, name="gate_row", tag="gate_row", align_bytes=64)
         identity = held.tile([P, P], F32, name="identity")
@@ -90,22 +97,27 @@ def tile_moe_res_lin_none_kernel(tc, xT, xr, w_words, w_scales, gate, offs, out)
                 landed[LANDING + r : LANDING + SCALE_ROWS * SPREAD : SCALE_ROWS].bitcast(I32),
                 by_row[r][0:SPREAD].bitcast(I32),
             )
-        source = {}
+        dealt = {}
         for g in range(SPREAD // PLANES):
             first = LANDING + GROUP_ROWS * g
             if first % QUADRANT == 0:
-                source[g] = landed[first : first + QUADRANT]
+                dealt[g] = held.tile([P, N], U8, name=f"dealt{g}", align_bytes=64)[:]
+                for q in range(QUADRANTS):
+                    nc.vector.tensor_copy(
+                        dealt[g][QUADRANT * q : QUADRANT * (q + 1), :].bitcast(I32),
+                        landed[first : first + QUADRANT, q, :].bitcast(I32),
+                    )
             else:
                 nc.sync.dma_start(
-                    lowered[top : top + GROUP_ROWS, g // 2].rearrange("p q n -> p (q n)").bitcast(I32),
-                    landed[first : first + GROUP_ROWS].rearrange("p q n -> p (q n)").bitcast(I32),
+                    lowered[top : top + GROUP_ROWS, :, g // 2, :].bitcast(I32),
+                    landed[first : first + GROUP_ROWS].bitcast(I32),
                 )
-                source[g] = lowered[top:P, g // 2]
-        for g in (0, 2, 1, 3):
-            for q in range(QUADRANTS):
-                nc.vector.tensor_copy(
-                    dealt[g][QUADRANT * q : QUADRANT * (q + 1), :].bitcast(I32), source[g][:, q, :].bitcast(I32)
-                )
+                dealt[g] = lowered[:, QUADRANTS - 1, g // 2, :]
+        for q in range(QUADRANTS - 1):
+            nc.vector.tensor_copy(
+                lowered[QUADRANT * q : QUADRANT * (q + 1), QUADRANTS - 1].rearrange("p g n -> p (g n)").bitcast(I32),
+                lowered[top:P, q].rearrange("p g n -> p (g n)").bitcast(I32),
+            )
 
         def w_scale(e, a, h):
             g, j = divmod(PASSES * e + a, PLANES)
@@ -141,6 +153,20 @@ def tile_moe_res_lin_none_kernel(tc, xT, xr, w_words, w_scales, gate, offs, out)
             return offsets[:, s0 // PER_COLUMN : s1 // PER_COLUMN]
 
         slot_words, slot_scales = {}, {}
+
+        def quantise(a, woven, s0, s1, tag=None):
+            words = held.tile([P, s1 - s0], U32, name=f"words{a}_{s0}", tag=tag or f"words{a}_{s0}", align_bytes=64)
+            scales = held.tile([P, s1 - s0], U8, name=f"scales{a}_{s0}", align_bytes=64)
+            base = max(b for b in woven if b <= s0)
+            nc.vector.quantize_mx(
+                out=words[:].bitcast(FP8X4),
+                scales=scales[:],
+                in_=woven[base][:, s0 - base : s1 - base, :].rearrange("p c t -> p (c t)"),
+            )
+            for e in range(s0 // C, s1 // C):
+                slot_words[a, e] = words[:, C * e - s0 : C * (e + 1) - s0]
+                slot_scales[a, e] = scales[:, C * e - s0 : C * (e + 1) - s0]
+
         for a in range(PASSES):
             parts = [(0, SLOTS)] if a < LAST else [(0, SLOTS // 2), (SLOTS // 2, SLOTS)]
             picked = {s0: held.tile([P, PACK, s1 - s0], F32, name=f"picked{a}_{s0}", align_bytes=64) for s0, s1 in parts}
@@ -166,18 +192,7 @@ def tile_moe_res_lin_none_kernel(tc, xT, xr, w_words, w_scales, gate, offs, out)
                         picked[base][:, :, s0 - base : s1 - base].rearrange("p t (c i) -> p c t i", i=4),
                     )
                 else:
-                    s0, s1 = where
-                    words = held.tile([P, s1 - s0], U32, name=f"words{a}_{s0}", align_bytes=64)
-                    scales = held.tile([P, s1 - s0], U8, name=f"scales{a}_{s0}", align_bytes=64)
-                    base = max(b for b in picked if b <= s0)
-                    nc.vector.quantize_mx(
-                        out=words[:].bitcast(FP8X4),
-                        scales=scales[:],
-                        in_=woven[base][:, s0 - base : s1 - base, :].rearrange("p c t -> p (c t)"),
-                    )
-                    for e in range(s0 // C, s1 // C):
-                        slot_words[a, e] = words[:, C * e - s0 : C * (e + 1) - s0]
-                        slot_scales[a, e] = scales[:, C * e - s0 : C * (e + 1) - s0]
+                    quantise(a, woven, *where)
 
         direct = held.tile([P, E * PASSES - SPREAD, N], U8, name="direct", tag="picked1_0", align_bytes=64)
         nc.vector.memset(direct[:].bitcast(I32), 0)
@@ -185,7 +200,7 @@ def tile_moe_res_lin_none_kernel(tc, xT, xr, w_words, w_scales, gate, offs, out)
         for r in range(SCALE_ROWS):
             nc.sync.dma_start(direct[r:P:QUADRANT].bitcast(I32), by_quadrant[r][:, SPREAD:, :].bitcast(I32))
         w_codes = held.tile([P, E * PASSES, N], U32, name="w_codes", tag="picked2_0", align_bytes=64)
-        w_loads = [[(0, 3), (3, PASSES)]] * 2 + [[(0, 3), (3, 4), (4, PASSES)]] * 2
+        w_loads = [[(0, 3), (3, PASSES)], [(2, PASSES), (0, 2)]] + [[(2, PASSES), (1, 2), (0, 1)]] * 2
         for e in range(E):
             for a0, a1 in w_loads[e]:
                 nc.sync.dma_start(
@@ -203,23 +218,24 @@ def tile_moe_res_lin_none_kernel(tc, xT, xr, w_words, w_scales, gate, offs, out)
                 sums[e, h] = psum.tile([P, C], F32, name=f"sum{e}{h}", tag=tag)
 
         for e in range(E):
-            for a0, a1 in w_loads[e]:
+            order = [sorted(range(a0, a1), reverse=e > 0) for a0, a1 in w_loads[e]]
+            for passes in order:
                 for h in range(HALVES):
-                    for a in range(a0, a1):
+                    for a in passes:
                         nc.tensor.matmul_mx(
                             out=sums[e, h][:],
                             lhsT=w_codes[:, PASSES * e + a, P * h : P * (h + 1)].bitcast(FP8X4),
                             lhsT_scale=w_scale(e, a, h),
                             rhs=slot_words[a, e].bitcast(FP8X4),
                             rhs_scale=slot_scales[a, e],
-                            start=(a == 0),
-                            stop=(a == LAST),
+                            start=(a == order[0][0]),
+                            stop=(a == order[-1][-1]),
                         )
 
         for e in range(E):
             product = []
             for h in range(HALVES):
-                product.append(held.tile([P, C], F32, name=f"product{e}{h}"))
+                product.append(held.tile([P, C], F32, name=f"product{e}{h}", align_bytes=64))
                 nc.vector.tensor_tensor(product[h][:], sums[e, h][:], gates[:, C * e : C * (e + 1)], MULT)
             nc.vector.tensor_copy(placed[0][:].indirect(entries(C * e, C * (e + 1))), product[0][:])
             nc.scalar.activation(placed[1][:].indirect(entries(C * e, C * (e + 1))), product[1][:], COPY)

@@ -33,17 +33,8 @@ SPREAD = 16
 LANDING = QUADRANT
 FREE_ROWS = 4
 
-LOADS = [[(0, 2), (2, 4)]] * 4 + [[(0, 2), (2, 3), (3, 4)]]
+LOADS = [[(0, 2), (2, 4)], [(0, 4)], [(0, 4)], [(0, 2), (2, 4)]] + [[(0, 2), (2, 3), (3, 4)]]
 STEADY = [
-    ("G", "S", 0, 0, 512),
-    ("G", "S", 1, 0, 256),
-    ("G", "V", 1, 256, 512),
-    ("G", "V", 2, 0, 512),
-    ("G", "S", 3, 0, 512),
-    ("W", "V", 0, 512),
-    ("Q", 0, 512),
-]
-OPENING = [
     ("G", "S", 0, 0, 512),
     ("G", "S", 1, 0, 512),
     ("G", "V", 2, 0, 512),
@@ -51,16 +42,38 @@ OPENING = [
     ("W", "V", 0, 512),
     ("Q", 0, 512),
 ]
+WHOLE = [
+    ("G", "S", 0, 0, 512),
+    ("G", "V", 2, 0, 512),
+    ("G", "S", 1, 0, 512),
+    ("G", "V", 3, 0, 512),
+    ("W", "V", 0, 512),
+    ("Q", 0, 512),
+]
+HALVED = [
+    ("G", "S", 0, 0, 256),
+    ("G", "S", 1, 0, 256),
+    ("G", "S", 0, 256, 512),
+    ("G", "S", 1, 256, 512),
+    ("G", "V", 2, 0, 256),
+    ("G", "S", 3, 0, 256),
+    ("G", "V", 2, 256, 512),
+    ("G", "S", 3, 256, 512),
+    ("W", "V", 0, 256),
+    ("W", "V", 256, 512),
+    ("Q", 0, 256),
+    ("Q", 256, 512),
+]
 FINAL = [
     ("G", "S", 0, 0, 256),
     ("G", "S", 1, 0, 256),
     ("G", "S", 0, 256, 512),
     ("G", "S", 1, 256, 512),
     ("G", "V", 2, 0, 256),
-    ("G", "S", 2, 256, 512),
+    ("G", "V", 2, 256, 384),
+    ("G", "S", 2, 384, 512),
     ("G", "V", 3, 0, 256),
-    ("G", "V", 3, 256, 384),
-    ("G", "S", 3, 384, 512),
+    ("G", "S", 3, 256, 512),
     ("W", "V", 0, 128),
     ("W", "V", 128, 256),
     ("Q", 0, 128),
@@ -69,7 +82,7 @@ FINAL = [
     ("W", "V", 256, 384),
     ("Q", 256, 512),
 ]
-STEPS = [OPENING, OPENING, OPENING, OPENING, FINAL]
+STEPS = [STEADY, WHOLE, WHOLE, HALVED, FINAL]
 
 
 def tile_moe_res_lin_none_kernel(tc, xT, xr, w_words, w_scales, gate, offs, out):
@@ -168,7 +181,7 @@ def tile_moe_res_lin_none_kernel(tc, xT, xr, w_words, w_scales, gate, offs, out)
                 slot_scales[a, e] = scales[:, C * e - s0 : C * (e + 1) - s0]
 
         for a in range(PASSES):
-            parts = [(0, SLOTS)] if a < LAST else [(0, SLOTS // 2), (SLOTS // 2, SLOTS)]
+            parts = [(0, SLOTS)] if a < LAST - 1 else [(0, SLOTS // 2), (SLOTS // 2, SLOTS)]
             picked = {s0: held.tile([P, PACK, s1 - s0], F32, name=f"picked{a}_{s0}", align_bytes=64) for s0, s1 in parts}
             woven = {
                 s0: held.tile([P, s1 - s0, PACK], BF16, name=f"woven{a}_{s0}", align_bytes=64) for s0, s1 in parts
@@ -194,19 +207,26 @@ def tile_moe_res_lin_none_kernel(tc, xT, xr, w_words, w_scales, gate, offs, out)
                 else:
                     quantise(a, woven, *where)
 
-        direct = held.tile([P, E * PASSES - SPREAD, N], U8, name="direct", tag="picked1_0", align_bytes=64)
+        w_loads = [[(0, LAST), (LAST, PASSES)], [(1, PASSES), (0, 1)]] + [[(2, PASSES), (1, 2), (0, 1)]] * 2
+        w_codes = {}
+
+        def load_words(experts, tag):
+            words = held.tile([P, len(experts) * PASSES, N], U32, name=f"w_codes{experts[0]}", tag=tag, align_bytes=64)
+            for i, e in enumerate(experts):
+                w_codes[e] = words[:, PASSES * i : PASSES * (i + 1), :]
+                for a0, a1 in w_loads[e]:
+                    nc.sync.dma_start(
+                        w_codes[e][:, a0:a1, :].bitcast(I32),
+                        w_words[e, a0:a1].rearrange("a p n r -> p a (n r)").bitcast(I32),
+                    )
+
+        load_words([0], "picked1_0")
+        direct = held.tile([P, E * PASSES - SPREAD, N], U8, name="direct", tag="picked2_0", align_bytes=64)
         nc.vector.memset(direct[:].bitcast(I32), 0)
         by_quadrant = w_scales.rearrange("e a (q r) n -> r q (e a) n", r=SCALE_ROWS)
         for r in range(SCALE_ROWS):
             nc.sync.dma_start(direct[r:P:QUADRANT].bitcast(I32), by_quadrant[r][:, SPREAD:, :].bitcast(I32))
-        w_codes = held.tile([P, E * PASSES, N], U32, name="w_codes", tag="picked2_0", align_bytes=64)
-        w_loads = [[(0, 3), (3, PASSES)], [(2, PASSES), (0, 2)]] + [[(2, PASSES), (1, 2), (0, 1)]] * 2
-        for e in range(E):
-            for a0, a1 in w_loads[e]:
-                nc.sync.dma_start(
-                    w_codes[:, PASSES * e + a0 : PASSES * e + a1, :].bitcast(I32),
-                    w_words[e, a0:a1].rearrange("a p n r -> p a (n r)").bitcast(I32),
-                )
+        load_words([1, 2, 3], "woven2_0")
         residual = held.tile([P, HALVES, T], F32, name="residual", tag="picked3_0", align_bytes=64)
         for h in range(HALVES):
             nc.sync.dma_start(residual[:, h, :], xr[P * h : P * (h + 1), :])
@@ -224,7 +244,7 @@ def tile_moe_res_lin_none_kernel(tc, xT, xr, w_words, w_scales, gate, offs, out)
                     for a in passes:
                         nc.tensor.matmul_mx(
                             out=sums[e, h][:],
-                            lhsT=w_codes[:, PASSES * e + a, P * h : P * (h + 1)].bitcast(FP8X4),
+                            lhsT=w_codes[e][:, a, P * h : P * (h + 1)].bitcast(FP8X4),
                             lhsT_scale=w_scale(e, a, h),
                             rhs=slot_words[a, e].bitcast(FP8X4),
                             rhs_scale=slot_scales[a, e],

@@ -47,8 +47,10 @@ WHOLE = [
     ("G", "V", 2, 0, 512),
     ("G", "S", 1, 0, 512),
     ("G", "V", 3, 0, 512),
-    ("W", "V", 0, 512),
-    ("Q", 0, 512),
+    ("W", "V", 0, 256),
+    ("W", "V", 256, 512),
+    ("Q", 0, 256),
+    ("Q", 256, 512),
 ]
 HALVED = [
     ("G", "S", 0, 0, 256),

@@ -209,17 +209,22 @@ def tile_moe_res_lin_none_kernel(tc, xT, xr, w_words, w_scales, gate, offs, out)
                 else:
                     quantise(a, woven, *where)
 
-        w_loads = [[(0, LAST), (LAST, PASSES)], [(1, PASSES), (0, 1)]] + [[(2, PASSES), (1, 2), (0, 1)]] * 2
+        w_loads = [
+            [(0, LAST, 0, N), (LAST, PASSES, 0, N)],
+            [(1, PASSES, 0, N), (0, 1, 0, N)],
+            [(2, PASSES, 0, N), (1, 2, 0, N), (0, 1, 0, N)],
+            [(3, PASSES, 0, N), (1, 3, 0, P), (0, 1, 0, P), (1, 3, P, N), (0, 1, P, N)],
+        ]
         w_codes = {}
 
         def load_words(experts, tag):
             words = held.tile([P, len(experts) * PASSES, N], U32, name=f"w_codes{experts[0]}", tag=tag, align_bytes=64)
             for i, e in enumerate(experts):
                 w_codes[e] = words[:, PASSES * i : PASSES * (i + 1), :]
-                for a0, a1 in w_loads[e]:
+                for a0, a1, n0, n1 in w_loads[e]:
                     nc.sync.dma_start(
-                        w_codes[e][:, a0:a1, :].bitcast(I32),
-                        w_words[e, a0:a1].rearrange("a p n r -> p a (n r)").bitcast(I32),
+                        w_codes[e][:, a0:a1, n0:n1].bitcast(I32),
+                        w_words[e, a0:a1, :, n0:n1].rearrange("a p n r -> p a (n r)").bitcast(I32),
                     )
 
         load_words([0], "picked1_0")
@@ -230,8 +235,8 @@ def tile_moe_res_lin_none_kernel(tc, xT, xr, w_words, w_scales, gate, offs, out)
             nc.sync.dma_start(direct[r:P:QUADRANT].bitcast(I32), by_quadrant[r][:, SPREAD:, :].bitcast(I32))
         load_words([1, 2, 3], "woven2_0")
         residual = held.tile([P, HALVES, T], F32, name="residual", tag="picked3_0", align_bytes=64)
-        for h in range(HALVES):
-            nc.sync.dma_start(residual[:, h, :], xr[P * h : P * (h + 1), :])
+        for h, c0, c1 in ((0, 0, T // 2), (0, T // 2, T), (1, 0, T)):
+            nc.sync.dma_start(residual[:, h, c0:c1], xr[P * h : P * (h + 1), c0:c1])
 
         sums = {}
         for e in range(E):
@@ -240,18 +245,18 @@ def tile_moe_res_lin_none_kernel(tc, xT, xr, w_words, w_scales, gate, offs, out)
                 sums[e, h] = psum.tile([P, C], F32, name=f"sum{e}{h}", tag=tag)
 
         for e in range(E):
-            order = [sorted(range(a0, a1), reverse=e > 0) for a0, a1 in w_loads[e]]
-            for passes in order:
-                for h in range(HALVES):
-                    for a in passes:
+            first, final = (0, LAST) if e == 0 else (LAST, 0)
+            for a0, a1, n0, n1 in w_loads[e]:
+                for h in range(n0 // P, n1 // P):
+                    for a in sorted(range(a0, a1), reverse=e > 0):
                         nc.tensor.matmul_mx(
                             out=sums[e, h][:],
                             lhsT=w_codes[e][:, a, P * h : P * (h + 1)].bitcast(FP8X4),
                             lhsT_scale=w_scale(e, a, h),
                             rhs=slot_words[a, e].bitcast(FP8X4),
                             rhs_scale=slot_scales[a, e],
-                            start=(a == order[0][0]),
-                            stop=(a == order[-1][-1]),
+                            start=(a == first),
+                            stop=(a == final),
                         )
 
         for e in range(E):

@@ -31,6 +31,7 @@ PLANES = 4
 GROUP_ROWS = PLANES * SCALE_ROWS
 SPREAD = 16
 LANDING = QUADRANT
+ALIGN = 256
 FREE_ROWS = 4
 
 LOADS = [[(0, 2), (2, 4)], [(0, 4)], [(0, 4)], [(0, 2), (2, 4)]] + [[(0, 2), (2, 3), (3, 4)]]
@@ -94,13 +95,13 @@ def tile_moe_res_lin_none_kernel(tc, xT, xr, w_words, w_scales, gate, offs, out)
         held = ctx.enter_context(tc.tile_pool(name="held", bufs=1))
         psum = ctx.enter_context(tc.psum_pool(name="psum", bufs=1))
 
-        offsets = lists.tile([P, SLOTS // PER_COLUMN], U16, name="offsets")
-        landed = held.tile([P, QUADRANTS, N], U8, name="landed", align_bytes=64)
-        lowered = held.tile([P, QUADRANTS, 2, N], U8, name="lowered", align_bytes=64)
-        gates = held.tile([P, SLOTS], F32, name="gates", tag="gates")
-        gate_row = held.tile([P, SLOTS // P], F32, name="gate_row", tag="gate_row", align_bytes=64)
-        identity = held.tile([P, P], F32, name="identity")
-        placed = [held.tile([P, T], F32, name=f"placed{h}") for h in range(HALVES)]
+        offsets = lists.tile([P, SLOTS // PER_COLUMN], U16, name="offsets", align_bytes=ALIGN)
+        landed = held.tile([P, QUADRANTS, N], U8, name="landed", align_bytes=ALIGN)
+        lowered = held.tile([P, QUADRANTS, 2, N], U8, name="lowered", align_bytes=ALIGN)
+        gates = held.tile([P, SLOTS], F32, name="gates", tag="gates", align_bytes=ALIGN)
+        gate_row = held.tile([P, SLOTS // P], F32, name="gate_row", tag="gate_row", align_bytes=ALIGN)
+        identity = held.tile([P, P], F32, name="identity", align_bytes=ALIGN)
+        placed = [held.tile([P, T], F32, name=f"placed{h}", align_bytes=ALIGN) for h in range(HALVES)]
 
         nc.sync.dma_start(gate_row[:], gate[0:1, :].rearrange("o (p i) -> (o p) i", p=P))
         top = P - QUADRANT
@@ -116,7 +117,7 @@ def tile_moe_res_lin_none_kernel(tc, xT, xr, w_words, w_scales, gate, offs, out)
         for g in range(SPREAD // PLANES):
             first = LANDING + GROUP_ROWS * g
             if first % QUADRANT == 0:
-                dealt[g] = held.tile([P, N], U8, name=f"dealt{g}", align_bytes=64)[:]
+                dealt[g] = held.tile([P, N], U8, name=f"dealt{g}", align_bytes=ALIGN)[:]
                 for q in range(QUADRANTS):
                     nc.vector.tensor_copy(
                         dealt[g][QUADRANT * q : QUADRANT * (q + 1), :].bitcast(I32),
@@ -150,12 +151,12 @@ def tile_moe_res_lin_none_kernel(tc, xT, xr, w_words, w_scales, gate, offs, out)
         nc.scalar.copy(gates[:].rearrange("m (p i) -> m p i", p=P), spread[:].rearrange("m i p -> m p i"))
 
         row = {}
-        later = held.tile([P, PACK * PASSES - FREE_ROWS, T], F32, name="later", tag="gate_row", align_bytes=64)
+        later = held.tile([P, PACK * PASSES - FREE_ROWS, T], F32, name="later", tag="gate_row", align_bytes=ALIGN)
         for a in range(PASSES):
             rows = xT[P * PACK * a : P * PACK * (a + 1), :].rearrange("(p t) w -> p t w", t=PACK)
             for t0, t1 in LOADS[a]:
                 if PACK * a + t0 < FREE_ROWS:
-                    raw = held.tile([P, t1 - t0, T], F32, name=f"raw{a}_{t0}")[:]
+                    raw = held.tile([P, t1 - t0, T], F32, name=f"raw{a}_{t0}", align_bytes=ALIGN)[:]
                 else:
                     raw = later[:, PACK * a + t0 - FREE_ROWS : PACK * a + t1 - FREE_ROWS, :]
                 nc.sync.dma_start(raw, rows[:, t0:t1, :])
@@ -170,8 +171,8 @@ def tile_moe_res_lin_none_kernel(tc, xT, xr, w_words, w_scales, gate, offs, out)
         slot_words, slot_scales = {}, {}
 
         def quantise(a, woven, s0, s1, tag=None):
-            words = held.tile([P, s1 - s0], U32, name=f"words{a}_{s0}", tag=tag or f"words{a}_{s0}", align_bytes=64)
-            scales = held.tile([P, s1 - s0], U8, name=f"scales{a}_{s0}", align_bytes=64)
+            words = held.tile([P, s1 - s0], U32, name=f"words{a}_{s0}", tag=tag or f"words{a}_{s0}", align_bytes=ALIGN)
+            scales = held.tile([P, s1 - s0], U8, name=f"scales{a}_{s0}", align_bytes=ALIGN)
             base = max(b for b in woven if b <= s0)
             nc.vector.quantize_mx(
                 out=words[:].bitcast(FP8X4),
@@ -184,9 +185,9 @@ def tile_moe_res_lin_none_kernel(tc, xT, xr, w_words, w_scales, gate, offs, out)
 
         for a in range(PASSES):
             parts = [(0, SLOTS)] if a < LAST - 1 else [(0, SLOTS // 2), (SLOTS // 2, SLOTS)]
-            picked = {s0: held.tile([P, PACK, s1 - s0], F32, name=f"picked{a}_{s0}", align_bytes=64) for s0, s1 in parts}
+            picked = {s0: held.tile([P, PACK, s1 - s0], F32, name=f"picked{a}_{s0}", align_bytes=ALIGN) for s0, s1 in parts}
             woven = {
-                s0: held.tile([P, s1 - s0, PACK], BF16, name=f"woven{a}_{s0}", align_bytes=64) for s0, s1 in parts
+                s0: held.tile([P, s1 - s0, PACK], BF16, name=f"woven{a}_{s0}", align_bytes=ALIGN) for s0, s1 in parts
             }
             for kind, *where in STEPS[a]:
                 if kind == "G":
@@ -218,7 +219,7 @@ def tile_moe_res_lin_none_kernel(tc, xT, xr, w_words, w_scales, gate, offs, out)
         w_codes = {}
 
         def load_words(experts, tag):
-            words = held.tile([P, len(experts) * PASSES, N], U32, name=f"w_codes{experts[0]}", tag=tag, align_bytes=64)
+            words = held.tile([P, len(experts) * PASSES, N], U32, name=f"w_codes{experts[0]}", tag=tag, align_bytes=ALIGN)
             for i, e in enumerate(experts):
                 w_codes[e] = words[:, PASSES * i : PASSES * (i + 1), :]
                 for a0, a1, n0, n1 in w_loads[e]:
@@ -228,13 +229,13 @@ def tile_moe_res_lin_none_kernel(tc, xT, xr, w_words, w_scales, gate, offs, out)
                     )
 
         load_words([0], "picked1_0")
-        direct = held.tile([P, E * PASSES - SPREAD, N], U8, name="direct", tag="picked2_0", align_bytes=64)
+        direct = held.tile([P, E * PASSES - SPREAD, N], U8, name="direct", tag="picked2_0", align_bytes=ALIGN)
         nc.vector.memset(direct[:].bitcast(I32), 0)
         by_quadrant = w_scales.rearrange("e a (q r) n -> r q (e a) n", r=SCALE_ROWS)
         for r in range(SCALE_ROWS):
             nc.sync.dma_start(direct[r:P:QUADRANT].bitcast(I32), by_quadrant[r][:, SPREAD:, :].bitcast(I32))
         load_words([1, 2, 3], "woven2_0")
-        residual = held.tile([P, HALVES, T], F32, name="residual", tag="picked3_0", align_bytes=64)
+        residual = held.tile([P, HALVES, T], F32, name="residual", tag="picked3_0", align_bytes=ALIGN)
         for h, c0, c1 in ((0, 0, T // 2), (0, T // 2, T), (1, 0, T)):
             nc.sync.dma_start(residual[:, h, c0:c1], xr[P * h : P * (h + 1), c0:c1])
 
@@ -262,7 +263,7 @@ def tile_moe_res_lin_none_kernel(tc, xT, xr, w_words, w_scales, gate, offs, out)
         for e in range(E):
             product = []
             for h in range(HALVES):
-                product.append(held.tile([P, C], F32, name=f"product{e}{h}", align_bytes=64))
+                product.append(held.tile([P, C], F32, name=f"product{e}{h}", align_bytes=ALIGN))
                 nc.vector.tensor_tensor(product[h][:], sums[e, h][:], gates[:, C * e : C * (e + 1)], MULT)
             nc.vector.tensor_copy(placed[0][:].indirect(entries(C * e, C * (e + 1))), product[0][:])
             nc.scalar.activation(placed[1][:].indirect(entries(C * e, C * (e + 1))), product[1][:], COPY)
@@ -270,6 +271,6 @@ def tile_moe_res_lin_none_kernel(tc, xT, xr, w_words, w_scales, gate, offs, out)
         for h in range(HALVES):
             for c0, c1 in ((0, T // 2), (T // 2, T)):
                 tag = "gates" if (h, c0) == (0, 0) else f"result{h}_{c0}"
-                result = held.tile([P, c1 - c0], F32, name=f"result{h}_{c0}", tag=tag)
+                result = held.tile([P, c1 - c0], F32, name=f"result{h}_{c0}", tag=tag, align_bytes=ALIGN)
                 nc.vector.tensor_tensor(result[:], placed[h][:, c0:c1], residual[:, h, c0:c1], ADD)
                 nc.sync.dma_start(out[P * h : P * (h + 1), c0:c1], result[:])

@@ -97,13 +97,12 @@ def tile_moe_res_lin_none_kernel(tc, xT, xr, w_words, w_scales, gate, offs, out)
 
         offsets = lists.tile([P, SLOTS // PER_COLUMN], U16, name="offsets", align_bytes=ALIGN)
         landed = held.tile([P, QUADRANTS, N], U8, name="landed", align_bytes=ALIGN)
-        lowered = held.tile([P, QUADRANTS, 2, N], U8, name="lowered", align_bytes=ALIGN)
+        lowered = held.tile([P, 2, QUADRANTS, N], U8, name="lowered", align_bytes=ALIGN)
         gates = held.tile([P, SLOTS], F32, name="gates", tag="gates", align_bytes=ALIGN)
         gate_row = held.tile([P, SLOTS // P], F32, name="gate_row", tag="gate_row", align_bytes=ALIGN)
         identity = held.tile([P, P], F32, name="identity", align_bytes=ALIGN)
         placed = [held.tile([P, T], F32, name=f"placed{h}", align_bytes=ALIGN) for h in range(HALVES)]
 
-        nc.sync.dma_start(gate_row[:], gate[0:1, :].rearrange("o (p i) -> (o p) i", p=P))
         top = P - QUADRANT
         nc.vector.memset(lowered[top:P].bitcast(I32), 0)
         by_row = w_scales.rearrange("e a (q r) n -> r (e a) q n", r=SCALE_ROWS)
@@ -113,6 +112,9 @@ def tile_moe_res_lin_none_kernel(tc, xT, xr, w_words, w_scales, gate, offs, out)
                 landed[LANDING + r : LANDING + SCALE_ROWS * SPREAD : SCALE_ROWS].bitcast(I32),
                 by_row[r][0:SPREAD].bitcast(I32),
             )
+        nc.sync.dma_start(gate_row[:], gate[0:1, :].rearrange("o (p i) -> (o p) i", p=P))
+        gate_columns = held.tile([P, SLOTS // P], F32, name="gate_columns", align_bytes=ALIGN)
+        nc.gpsimd.tensor_copy(gate_columns[:], gate_row[:])
         dealt = {}
         for g in range(SPREAD // PLANES):
             first = LANDING + GROUP_ROWS * g
@@ -125,15 +127,16 @@ def tile_moe_res_lin_none_kernel(tc, xT, xr, w_words, w_scales, gate, offs, out)
                     )
             else:
                 nc.sync.dma_start(
-                    lowered[top : top + GROUP_ROWS, :, g // 2, :].bitcast(I32),
+                    lowered[top : top + GROUP_ROWS, g // 2].bitcast(I32),
                     landed[first : first + GROUP_ROWS].bitcast(I32),
                 )
-                dealt[g] = lowered[:, QUADRANTS - 1, g // 2, :]
-        for q in range(QUADRANTS - 1):
-            nc.vector.tensor_copy(
-                lowered[QUADRANT * q : QUADRANT * (q + 1), QUADRANTS - 1].rearrange("p g n -> p (g n)").bitcast(I32),
-                lowered[top:P, q].rearrange("p g n -> p (g n)").bitcast(I32),
-            )
+                dealt[g] = lowered[:, g // 2, QUADRANTS - 1, :]
+        for i in range(2):
+            for q in range(QUADRANTS - 1):
+                nc.vector.tensor_copy(
+                    lowered[QUADRANT * q : QUADRANT * (q + 1), i, QUADRANTS - 1, :].bitcast(I32),
+                    lowered[top:P, i, q, :].bitcast(I32),
+                )
 
         def w_scale(e, a, h):
             g, j = divmod(PASSES * e + a, PLANES)
@@ -147,7 +150,7 @@ def tile_moe_res_lin_none_kernel(tc, xT, xr, w_words, w_scales, gate, offs, out)
 
         spread = psum.tile([P, SLOTS // P, P], F32, name="spread", tag="last")
         for i in range(SLOTS // P):
-            nc.tensor.transpose(spread[:, i, :], gate_row[:, i : i + 1].to_broadcast([P, P]), identity[:])
+            nc.tensor.transpose(spread[:, i, :], gate_columns[:, i : i + 1].to_broadcast([P, P]), identity[:])
         nc.scalar.copy(gates[:].rearrange("m (p i) -> m p i", p=P), spread[:].rearrange("m i p -> m p i"))
 
         row = {}
@@ -211,8 +214,8 @@ def tile_moe_res_lin_none_kernel(tc, xT, xr, w_words, w_scales, gate, offs, out)
                     quantise(a, woven, *where)
 
         w_loads = [
-            [(0, LAST, 0, N), (LAST, PASSES, 0, N)],
-            [(1, PASSES, 0, N), (0, 1, 0, N)],
+            [(0, 3, 0, N), (3, PASSES, 0, N)],
+            [(2, PASSES, 0, N), (0, 2, 0, N)],
             [(2, PASSES, 0, N), (1, 2, 0, N), (0, 1, 0, N)],
             [(3, PASSES, 0, N), (1, 3, 0, P), (0, 1, 0, P), (1, 3, P, N), (0, 1, P, N)],
         ]
@@ -236,7 +239,7 @@ def tile_moe_res_lin_none_kernel(tc, xT, xr, w_words, w_scales, gate, offs, out)
             nc.sync.dma_start(direct[r:P:QUADRANT].bitcast(I32), by_quadrant[r][:, SPREAD:, :].bitcast(I32))
         load_words([1, 2, 3], "woven2_0")
         residual = held.tile([P, HALVES, T], F32, name="residual", tag="picked3_0", align_bytes=ALIGN)
-        for h, c0, c1 in ((0, 0, T // 2), (0, T // 2, T), (1, 0, T)):
+        for h, c0, c1 in ((0, 0, T), (1, 0, T // 2), (1, T // 2, T)):
             nc.sync.dma_start(residual[:, h, c0:c1], xr[P * h : P * (h + 1), c0:c1])
 
         sums = {}

from contextlib import ExitStack

import concourse.mybir as mybir
from concourse.masks import make_identity

K, T, E, C, N = 2560, 1024, 4, 128, 256
SLOTS = E * C
FLOPS = 2 * K * SLOTS * N

F32 = mybir.dt.float32
BF16 = mybir.dt.bfloat16
I32 = mybir.dt.int32
U32 = mybir.dt.uint32
U16 = mybir.dt.uint16
U8 = mybir.dt.uint8
FP8X4 = mybir.dt.float8_e4m3fn_x4
MULT = mybir.AluOpType.mult
ADD = mybir.AluOpType.add
COPY = mybir.ActivationFunctionType.Copy

P = 128
PACK = 4
PASSES = K // (P * PACK)
LAST = PASSES - 1
HALVES = N // P
PER_COLUMN = 16
QUADRANT = 32
QUADRANTS = P // QUADRANT
SCALE_ROWS = 4
PLANES = 4
GROUP_ROWS = PLANES * SCALE_ROWS
SPREAD = 16
LANDING = QUADRANT
ALIGN = 256
FREE_ROWS = 4

LOADS = [[(0, 2), (2, 4)], [(0, 4)], [(0, 4)], [(0, 2), (2, 4)]] + [[(0, 2), (2, 3), (3, 4)]]
STEADY = [
    ("G", "S", 0, 0, 512),
    ("G", "S", 1, 0, 512),
    ("G", "V", 2, 0, 512),
    ("G", "S", 3, 0, 512),
    ("W", "V", 0, 512),
    ("Q", 0, 512),
]
WHOLE = [
    ("G", "S", 0, 0, 512),
    ("G", "V", 2, 0, 512),
    ("G", "S", 1, 0, 512),
    ("G", "V", 3, 0, 512),
    ("W", "V", 0, 256),
    ("W", "V", 256, 512),
    ("Q", 0, 256),
    ("Q", 256, 512),
]
HALVED = [
    ("G", "S", 0, 0, 256),
    ("G", "S", 1, 0, 256),
    ("G", "S", 0, 256, 512),
    ("G", "S", 1, 256, 512),
    ("G", "V", 2, 0, 256),
    ("G", "S", 3, 0, 256),
    ("G", "V", 2, 256, 512),
    ("G", "S", 3, 256, 512),
    ("W", "V", 0, 256),
    ("W", "V", 256, 512),
    ("Q", 0, 256),
    ("Q", 256, 512),
]
FINAL = [
    ("G", "S", 0, 0, 256),
    ("G", "S", 1, 0, 256),
    ("G", "S", 0, 256, 512),
    ("G", "S", 1, 256, 512),
    ("G", "V", 2, 0, 256),
    ("G", "V", 2, 256, 384),
    ("G", "S", 2, 384, 512),
    ("G", "V", 3, 0, 256),
    ("G", "S", 3, 256, 512),
    ("W", "V", 0, 128),
    ("W", "V", 128, 256),
    ("Q", 0, 128),
    ("Q", 128, 256),
    ("W", "S", 384, 512),
    ("W", "V", 256, 384),
    ("Q", 256, 512),
]
STEPS = [STEADY, WHOLE, WHOLE, HALVED, FINAL]


def tile_moe_res_lin_none_kernel(tc, xT, xr, w_words, w_scales, gate, offs, out):
    nc = tc.nc
    with ExitStack() as ctx:
        lists = ctx.enter_context(tc.tile_pool(name="lists", bufs=1))
        held = ctx.enter_context(tc.tile_pool(name="held", bufs=1))
        psum = ctx.enter_context(tc.psum_pool(name="psum", bufs=1))

        offsets = lists.tile([P, SLOTS // PER_COLUMN], U16, name="offsets", align_bytes=ALIGN)
        landed = held.tile([P, QUADRANTS, N], U8, name="landed", align_bytes=ALIGN)
        lowered = held.tile([P, 2, QUADRANTS, N], U8, name="lowered", align_bytes=ALIGN)
        gates = held.tile([P, SLOTS], F32, name="gates", tag="gates", align_bytes=ALIGN)
        gate_row = held.tile([P, SLOTS // P], F32, name="gate_row", tag="gate_row", align_bytes=ALIGN)
        identity = held.tile([P, P], F32, name="identity", align_bytes=ALIGN)
        placed = [held.tile([P, T], F32, name=f"placed{h}", align_bytes=ALIGN) for h in range(HALVES)]

        top = P - QUADRANT
        nc.vector.memset(lowered[top:P].bitcast(I32), 0)
        by_row = w_scales.rearrange("e a (q r) n -> r (e a) q n", r=SCALE_ROWS)
        for r in range(SCALE_ROWS):
            queue = nc.scalar if r < SCALE_ROWS // 2 else nc.sync
            queue.dma_start(
                landed[LANDING + r : LANDING + SCALE_ROWS * SPREAD : SCALE_ROWS].bitcast(I32),
                by_row[r][0:SPREAD].bitcast(I32),
            )
        nc.sync.dma_start(gate_row[:], gate[0:1, :].rearrange("o (p i) -> (o p) i", p=P))
        gate_columns = held.tile([P, SLOTS // P], F32, name="gate_columns", align_bytes=ALIGN)
        nc.gpsimd.tensor_copy(gate_columns[:], gate_row[:])
        dealt = {}
        for g in range(SPREAD // PLANES):
            first = LANDING + GROUP_ROWS * g
            if first % QUADRANT == 0:
                dealt[g] = held.tile([P, N], U8, name=f"dealt{g}", align_bytes=ALIGN)[:]
                for q in range(QUADRANTS):
                    nc.vector.tensor_copy(
                        dealt[g][QUADRANT * q : QUADRANT * (q + 1), :].bitcast(I32),
                        landed[first : first + QUADRANT, q, :].bitcast(I32),
                    )
            else:
                nc.sync.dma_start(
                    lowered[top : top + GROUP_ROWS, g // 2].bitcast(I32),
                    landed[first : first + GROUP_ROWS].bitcast(I32),
                )
                dealt[g] = lowered[:, g // 2, QUADRANTS - 1, :]
        for i in range(2):
            for q in range(QUADRANTS - 1):
                nc.vector.tensor_copy(
                    lowered[QUADRANT * q : QUADRANT * (q + 1), i, QUADRANTS - 1, :].bitcast(I32),
                    lowered[top:P, i, q, :].bitcast(I32),
                )

        def w_scale(e, a, h):
            g, j = divmod(PASSES * e + a, PLANES)
            if g < len(dealt):
                return dealt[g][SCALE_ROWS * j :, P * h : P * (h + 1)]
            return direct[:, j, P * h : P * (h + 1)]

        make_identity(nc, identity[:])
        nc.gpsimd.memset(placed[0][:], 0.0)
        nc.scalar.copy(placed[1][:], placed[0][:])

        spread = psum.tile([P, SLOTS // P, P], F32, name="spread", tag="last")
        for i in range(SLOTS // P):
            nc.tensor.transpose(spread[:, i, :], gate_columns[:, i : i + 1].to_broadcast([P, P]), identity[:])
        nc.scalar.copy(gates[:].rearrange("m (p i) -> m p i", p=P), spread[:].rearrange("m i p -> m p i"))

        row = {}
        later = held.tile([P, PACK * PASSES - FREE_ROWS, T], F32, name="later", tag="gate_row", align_bytes=ALIGN)
        for a in range(PASSES):
            rows = xT[P * PACK * a : P * PACK * (a + 1), :].rearrange("(p t) w -> p t w", t=PACK)
            for t0, t1 in LOADS[a]:
                if PACK * a + t0 < FREE_ROWS:
                    raw = held.tile([P, t1 - t0, T], F32, name=f"raw{a}_{t0}", align_bytes=ALIGN)[:]
                else:
                    raw = later[:, PACK * a + t0 - FREE_ROWS : PACK * a + t1 - FREE_ROWS, :]
                nc.sync.dma_start(raw, rows[:, t0:t1, :])
                for t in range(t0, t1):
                    row[a, t] = raw[:, t - t0, :]
                if (a, t0) == (0, 0):
                    nc.sync.dma_start(offsets[:], offs)

        def entries(s0, s1):
            return offsets[:, s0 // PER_COLUMN : s1 // PER_COLUMN]

        slot_words, slot_scales = {}, {}

        def quantise(a, woven, s0, s1, tag=None):
            words = held.tile([P, s1 - s0], U32, name=f"words{a}_{s0}", tag=tag or f"words{a}_{s0}", align_bytes=ALIGN)
            scales = held.tile([P, s1 - s0], U8, name=f"scales{a}_{s0}", align_bytes=ALIGN)
            base = max(b for b in woven if b <= s0)
            nc.vector.quantize_mx(
                out=words[:].bitcast(FP8X4),
                scales=scales[:],
                in_=woven[base][:, s0 - base : s1 - base, :].rearrange("p c t -> p (c t)"),
            )
            for e in range(s0 // C, s1 // C):
                slot_words[a, e] = words[:, C * e - s0 : C * (e + 1) - s0]
                slot_scales[a, e] = scales[:, C * e - s0 : C * (e + 1) - s0]

        for a in range(PASSES):
            parts = [(0, SLOTS)] if a < LAST - 1 else [(0, SLOTS // 2), (SLOTS // 2, SLOTS)]
            picked = {s0: held.tile([P, PACK, s1 - s0], F32, name=f"picked{a}_{s0}", align_bytes=ALIGN) for s0, s1 in parts}
            woven = {
                s0: held.tile([P, s1 - s0, PACK], BF16, name=f"woven{a}_{s0}", align_bytes=ALIGN) for s0, s1 in parts
            }
            for kind, *where in STEPS[a]:
                if kind == "G":
                    engine, t, s0, s1 = where
                    base = max(b for b in picked if b <= s0)
                    target = picked[base][:, t, s0 - base : s1 - base]
                    window = row[a, t].indirect(entries(s0, s1))
                    if engine == "S":
                        nc.scalar.activation(target, window, COPY)
                    else:
                        nc.vector.tensor_copy(target, window)
                elif kind == "W":
                    engine, s0, s1 = where
                    copy = nc.scalar.copy if engine == "S" else nc.vector.tensor_copy
                    base = max(b for b in picked if b <= s0)
                    copy(
                        woven[base][:, s0 - base : s1 - base, :].rearrange("p (c i) t -> p c t i", i=4),
                        picked[base][:, :, s0 - base : s1 - base].rearrange("p t (c i) -> p c t i", i=4),
                    )
                else:
                    quantise(a, woven, *where)

        w_loads = [
            [(0, 3, 0, N), (3, PASSES, 0, N)],
            [(2, PASSES, 0, N), (0, 2, 0, N)],
            [(2, PASSES, 0, N), (1, 2, 0, N), (0, 1, 0, N)],
            [(3, PASSES, 0, N), (1, 3, 0, P), (0, 1, 0, P), (1, 3, P, N), (0, 1, P, N)],
        ]
        w_codes = {}

        def load_words(experts, tag):
            words = held.tile([P, len(experts) * PASSES, N], U32, name=f"w_codes{experts[0]}", tag=tag, align_bytes=ALIGN)
            for i, e in enumerate(experts):
                w_codes[e] = words[:, PASSES * i : PASSES * (i + 1), :]
                for a0, a1, n0, n1 in w_loads[e]:
                    nc.sync.dma_start(
                        w_codes[e][:, a0:a1, n0:n1].bitcast(I32),
                        w_words[e, a0:a1, :, n0:n1].rearrange("a p n r -> p a (n r)").bitcast(I32),
                    )

        load_words([0], "picked1_0")
        direct = held.tile([P, E * PASSES - SPREAD, N], U8, name="direct", tag="picked2_0", align_bytes=ALIGN)
        nc.vector.memset(direct[:].bitcast(I32), 0)
        by_quadrant = w_scales.rearrange("e a (q r) n -> r q (e a) n", r=SCALE_ROWS)
        for r in range(SCALE_ROWS):
            nc.sync.dma_start(direct[r:P:QUADRANT].bitcast(I32), by_quadrant[r][:, SPREAD:, :].bitcast(I32))
        load_words([1, 2, 3], "woven2_0")
        residual = held.tile([P, HALVES, T], F32, name="residual", tag="picked3_0", align_bytes=ALIGN)
        for h, c0, c1 in ((0, 0, T), (1, 0, T // 2), (1, T // 2, T)):
            nc.sync.dma_start(residual[:, h, c0:c1], xr[P * h : P * (h + 1), c0:c1])

        sums = {}
        for e in range(E):
            for h in range(HALVES):
                tag = "last" if (e, h) == (E - 1, HALVES - 1) else f"sum{e}{h}"
                sums[e, h] = psum.tile([P, C], F32, name=f"sum{e}{h}", tag=tag)

        for e in range(E):
            first, final = (0, LAST) if e == 0 else (LAST, 0)
            for a0, a1, n0, n1 in w_loads[e]:
                for h in range(n0 // P, n1 // P):
                    for a in sorted(range(a0, a1), reverse=e > 0):
                        nc.tensor.matmul_mx(
                            out=sums[e, h][:],
                            lhsT=w_codes[e][:, a, P * h : P * (h + 1)].bitcast(FP8X4),
                            lhsT_scale=w_scale(e, a, h),
                            rhs=slot_words[a, e].bitcast(FP8X4),
                            rhs_scale=slot_scales[a, e],
                            start=(a == first),
                            stop=(a == final),
                        )

        for e in range(E):
            product = []
            for h in range(HALVES):
                product.append(held.tile([P, C], F32, name=f"product{e}{h}", align_bytes=ALIGN))
                nc.vector.tensor_tensor(product[h][:], sums[e, h][:], gates[:, C * e : C * (e + 1)], MULT)
            nc.vector.tensor_copy(placed[0][:].indirect(entries(C * e, C * (e + 1))), product[0][:])
            nc.scalar.activation(placed[1][:].indirect(entries(C * e, C * (e + 1))), product[1][:], COPY)

        for h in range(HALVES):
            for c0, c1 in ((0, T // 2), (T // 2, T)):
                tag = "gates" if (h, c0) == (0, 0) else f"result{h}_{c0}"
                result = held.tile([P, c1 - c0], F32, name=f"result{h}_{c0}", tag=tag, align_bytes=ALIGN)
                nc.vector.tensor_tensor(result[:], placed[h][:, c0:c1], residual[:, h, c0:c1], ADD)
                nc.sync.dma_start(out[P * h : P * (h + 1), c0:c1], result[:])
